import numpy as np
import ml_dtypes


def mxq(x, axis, fmt="e4m3"):
    dtype, down = {"e4m3": (ml_dtypes.float8_e4m3fn, 7), "e5m2": (ml_dtypes.float8_e5m2, 14)}[fmt]
    v = np.moveaxis(np.asarray(x, np.float32).astype(ml_dtypes.bfloat16).astype(np.float64), axis, -1)
    blocks = v.reshape(v.shape[:-1] + (-1, 32))
    amax = np.abs(blocks).max(-1, keepdims=True)
    byte = np.maximum(np.where(amax > 0, np.frexp(amax)[1] - 1 + 127, 0) - down, 1)
    scale = np.exp2(byte - 127.0)
    codes = (blocks / scale).astype(np.float32).astype(dtype).astype(np.float64)
    return np.moveaxis((codes * scale).reshape(v.shape), -1, axis)


WIDE = False


def mx_kscale(k):
    if not WIDE:
        return np.ones(k)
    levels = np.array([10, -10, 5, -5, 0])
    if k % 512:
        return np.exp2(np.random.permutation(np.resize(levels, k // 32))).repeat(32)
    a = np.empty((k // 512, 16))
    for p in range(k // 512):
        a[p, :8] = np.random.permutation(np.resize(levels, 8))
        for g in range(8):
            far = levels[np.abs(levels - a[p, g]) >= 10]
            a[p, g + 8] = far[np.random.randint(len(far))]
    return np.exp2(a.ravel()).repeat(32)


def f64(x):
    return np.asarray(x).astype(np.float64)


def striped(idx):
    return np.tile(idx.reshape(-1, 16).T, (8, 1)).astype(np.uint16)


def unstriped(offs):
    return offs[:16].T.reshape(-1).astype(np.int64)


def pack_weight(w):
    k, n = w.shape
    w = f64(np.asarray(w, np.float32).astype(ml_dtypes.bfloat16)).reshape(k // 32, 32, n)
    amax = np.abs(w).max(1)
    byte = np.clip(np.where(amax > 0, np.frexp(amax)[1] - 1 + 127 - 7, 1), 1, 254)
    scaled = (w * np.exp2(127.0 - byte)[:, None, :]).reshape(k, n).astype(np.float32)
    words = np.ascontiguousarray(scaled.reshape(k // 512, 128, 4, n).transpose(0, 1, 3, 2)).astype(ml_dtypes.float8_e4m3fn).view(np.uint8)
    return words, np.ascontiguousarray(byte.astype(np.uint8).reshape(k // 512, 16, n))


def unpack_weight(words, scales):
    g, p, n, _ = words.shape
    vals = np.ascontiguousarray(words).view(ml_dtypes.float8_e4m3fn).astype(np.float64) * np.repeat(np.exp2(scales.astype(np.float64) - 127.0), 8, axis=1)[..., None]
    return vals.transpose(0, 1, 3, 2).reshape(g * 512, n)


K, T, S, V, N = 1024, 2048, 512, 128, 128


def setup_inputs():
    n = np.random.standard_normal
    s = mx_kscale(K)[:, None]
    packed_w1 = pack_weight(n((K, N)) / np.sqrt(K) / s)
    packed_w2 = pack_weight(n((K, N)) / np.sqrt(K) / s)
    return {
        "xT": (n((K, T)) * s).astype(np.float32),
        "w1_words": packed_w1[0],
        "w1_scales": packed_w1[1],
        "w2_words": packed_w2[0],
        "w2_scales": packed_w2[1],
        "offs": striped(np.random.permutation(T)[:S]),
    }


def reference(xT, w1_words, w1_scales, w2_words, w2_scales, offs):
    xq = mxq(f64(xT)[:, unstriped(offs)], 0, "e4m3")
    e = np.exp(unpack_weight(w1_words, w1_scales).T @ xq)
    h = unpack_weight(w2_words, w2_scales).T @ xq
    num = e[:, :V] * h[:, :V] + e[:, V:2 * V] * h[:, V:2 * V] + e[:, 2 * V:3 * V] * h[:, 2 * V:3 * V] + e[:, 3 * V:4 * V] * h[:, 3 * V:4 * V]
    den = e[:, :V] + e[:, V:2 * V] + e[:, 2 * V:3 * V] + e[:, 3 * V:4 * V]
    return num / den

@@ -1,0 +1,114 @@
+from contextlib import ExitStack
+
+import concourse.mybir as mybir
+
+K, T, S, V, N = 1024, 2048, 512, 128, 128
+FLOPS = 2 * 2 * K * N * S
+
+F32 = mybir.dt.float32
+BF16 = mybir.dt.bfloat16
+U32 = mybir.dt.uint32
+I32 = mybir.dt.int32
+U16 = mybir.dt.uint16
+U8 = mybir.dt.uint8
+FP8X4 = mybir.dt.float8_e4m3fn_x4
+ALU = mybir.AluOpType
+ACT = mybir.ActivationFunctionType
+AX = mybir.AxisListType
+
+P = 128
+PACK = 4
+PASSES = K // (P * PACK)
+D = S // V
+HALVES = 2
+VH = V // HALVES
+HC = D * VH
+
+
+def tile_picked_apool_none_e_kernel(tc, xT, w1_words, w1_scales, w2_words, w2_scales, offs, out):
+    nc = tc.nc
+    with ExitStack() as ctx:
+        keep = ctx.enter_context(tc.tile_pool(name="keep", bufs=1))
+        psum = ctx.enter_context(tc.psum_pool(name="psum", bufs=1))
+
+        offsets = keep.tile([P, S // 16], U16, name="offsets")
+        planes = [keep.tile([P, T], F32, name="plane%d" % i, align_bytes=64) for i in range(PASSES * PACK)]
+        x_rows = xT.rearrange("(z p j) t -> z j p t", z=PASSES, j=PACK)
+        w_words = [keep.tile([P, PASSES, N], I32, name="w_words%d" % i, align_bytes=64) for i in range(2)]
+        w_scales = keep.tile([P, 2, PASSES, N], U8, name="w_scales", align_bytes=64)
+
+        warm = keep.tile([P, 8], F32, name="warm")
+        warm_out = keep.tile([P, 8], F32, name="warm_out")
+        nc.gpsimd.memset(warm[:], 0.0)
+        nc.scalar.activation(out=warm_out[:], in_=warm[:], func=ACT.Exp)
+
+        nc.gpsimd.memset(w_scales[:].rearrange("p a z n -> p (a z n)").bitcast(I32), 0)
+        for a, scales in enumerate((w1_scales, w2_scales)):
+            for q in range(4):
+                nc.gpsimd.dma_start(
+                    out=w_scales[32 * q : 32 * q + 4, a, :, :].bitcast(I32),
+                    in_=scales[:, 4 * q : 4 * q + 4, :].rearrange("z r n -> r z n").bitcast(I32),
+                )
+
+        for i in range(PASSES * PACK):
+            nc.sync.dma_start(out=planes[i][:], in_=x_rows[i // PACK, i % PACK])
+            if i == 0:
+                nc.sync.dma_start(offsets[:], offs)
+            if i == 2:
+                for a, words in enumerate((w1_words, w2_words)):
+                    nc.sync.dma_start(out=w_words[a][:], in_=words.rearrange("z p n r -> p z (n r)").bitcast(I32))
+
+        banks = [[psum.tile([P, HC], F32, name="bank%d%d" % (a, h)) for h in range(HALVES)] for a in range(2)]
+        for z in range(PASSES):
+            picked = keep.tile([P, HALVES, D, VH, PACK], BF16, name="picked%d" % z, align_bytes=64)
+            for j in range(PACK):
+                nc.vector.tensor_copy(
+                    out=picked[:, :, :, :, j].rearrange("p h d v -> p d h v"),
+                    in_=planes[PACK * z + j][:].indirect(offsets[:]),
+                )
+            codes = [keep.tile([P, HC], U32, name="codes%d%d" % (z, h), align_bytes=64) for h in range(HALVES)]
+            x_scales = [keep.tile([P, HC], U8, name="x_scales%d%d" % (z, h), align_bytes=64) for h in range(HALVES)]
+            for h in range(HALVES):
+                nc.vector.quantize_mx(
+                    out=codes[h][:].bitcast(FP8X4),
+                    scales=x_scales[h][:],
+                    in_=picked[:, h].rearrange("p d v j -> p (d v j)"),
+                )
+            for a in range(2):
+                for h in range(HALVES):
+                    nc.tensor.matmul_mx(
+                        out=banks[a][h][:],
+                        lhsT=w_words[a][:, z, :].bitcast(FP8X4),
+                        lhsT_scale=w_scales[:, a, z, :],
+                        rhs=codes[h][:].bitcast(FP8X4),
+                        rhs_scale=x_scales[h][:],
+                        start=(z == 0),
+                        stop=(z == PASSES - 1),
+                    )
+
+        top = [keep.tile([P, VH], F32, name="top%d" % h) for h in range(HALVES)]
+        shifted = [keep.tile([P, D, VH], F32, name="shifted%d" % h) for h in range(HALVES)]
+        e = [keep.tile([P, D, VH], F32, name="e%d" % h) for h in range(HALVES)]
+        eh = [keep.tile([P, D, VH], F32, name="eh%d" % h) for h in range(HALVES)]
+        den = keep.tile([P, HALVES, VH], F32, name="den")
+        num = keep.tile([P, HALVES, VH], F32, name="num")
+        for h in range(HALVES):
+            nc.vector.tensor_reduce(out=top[h][:], in_=banks[0][h][:].rearrange("p (d v) -> p v d", d=D), axis=AX.X, op=ALU.max)
+        for h in range(HALVES):
+            nc.vector.tensor_tensor(
+                out=shifted[h][:],
+                in0=banks[0][h][:].rearrange("p (d v) -> p d v", d=D),
+                in1=top[h][:].unsqueeze(1).to_broadcast([P, D, VH]),
+                op=ALU.subtract,
+            )
+            nc.scalar.activation(out=e[h][:], in_=shifted[h][:], func=ACT.Exp)
+        for h in range(HALVES):
+            nc.vector.tensor_reduce(out=den[:, h, :], in_=e[h][:].rearrange("p d v -> p v d"), axis=AX.X, op=ALU.add)
+            nc.vector.tensor_tensor(out=eh[h][:], in0=banks[1][h][:].rearrange("p (d v) -> p d v", d=D), in1=e[h][:], op=ALU.mult)
+        inv = keep.tile([P, V], F32, name="inv")
+        nc.vector.reciprocal(out=inv[:], in_=den[:].rearrange("p h v -> p (h v)"))
+        for h in range(HALVES):
+            nc.vector.tensor_reduce(out=num[:, h, :], in_=eh[h][:].rearrange("p d v -> p v d"), axis=AX.X, op=ALU.add)
+        result = keep.tile([P, V], F32, name="result")
+        nc.vector.tensor_tensor(out=result[:], in0=num[:].rearrange("p h v -> p (h v)"), in1=inv[:], op=ALU.mult)
+        nc.sync.dma_start(out=out, in_=result[:])

@@ -22,6 +22,9 @@ PASSES = K // (P * PACK)
 D = S // V
 HALVES = 2
 VH = V // HALVES
+QUARTERS = 4
+VQ = V // QUARTERS
+QC = D * VQ
 HC = D * VH
 
 
@@ -39,13 +42,13 @@ def tile_picked_apool_none_e_kernel(tc, xT, w1_words, w1_scales, w2_words, w2_sc
 
         warm = keep.tile([P, 8], F32, name="warm")
         warm_out = keep.tile([P, 8], F32, name="warm_out")
-        nc.gpsimd.memset(warm[:], 0.0)
+        nc.vector.memset(warm[:], 0.0)
         nc.scalar.activation(out=warm_out[:], in_=warm[:], func=ACT.Exp)
 
-        nc.gpsimd.memset(w_scales[:].rearrange("p a z n -> p (a z n)").bitcast(I32), 0)
+        nc.vector.memset(w_scales[:].rearrange("p a z n -> p (a z n)").bitcast(I32), 0)
         for a, scales in enumerate((w1_scales, w2_scales)):
             for q in range(4):
-                nc.gpsimd.dma_start(
+                nc.scalar.dma_start(
                     out=w_scales[32 * q : 32 * q + 4, a, :, :].bitcast(I32),
                     in_=scales[:, 4 * q : 4 * q + 4, :].rearrange("z r n -> r z n").bitcast(I32),
                 )
@@ -54,61 +57,85 @@ def tile_picked_apool_none_e_kernel(tc, xT, w1_words, w1_scales, w2_words, w2_sc
             nc.sync.dma_start(out=planes[i][:], in_=x_rows[i // PACK, i % PACK])
             if i == 0:
                 nc.sync.dma_start(offsets[:], offs)
-            if i == 2:
-                for a, words in enumerate((w1_words, w2_words)):
-                    nc.sync.dma_start(out=w_words[a][:], in_=words.rearrange("z p n r -> p z (n r)").bitcast(I32))
+        for a, words in enumerate((w1_words, w2_words)):
+            nc.sync.dma_start(out=w_words[a][:], in_=words.rearrange("z p n r -> p z (n r)").bitcast(I32))
 
-        banks = [[psum.tile([P, HC], F32, name="bank%d%d" % (a, h)) for h in range(HALVES)] for a in range(2)]
+        s_banks = [psum.tile([P, D, VQ], F32, name="s_bank%d" % q) for q in range(QUARTERS)]
+        h_banks = [psum.tile([P, HC], F32, name="h_bank%d" % h) for h in range(HALVES)]
         for z in range(PASSES):
-            picked = keep.tile([P, HALVES, D, VH, PACK], BF16, name="picked%d" % z, align_bytes=64)
+            picked = keep.tile([P, QUARTERS, D, VQ, PACK], BF16, name="picked%d" % z, align_bytes=64)
             for j in range(PACK):
                 nc.vector.tensor_copy(
-                    out=picked[:, :, :, :, j].rearrange("p h d v -> p d h v"),
+                    out=picked[:, :, :, :, j].rearrange("p q d v -> p d q v"),
                     in_=planes[PACK * z + j][:].indirect(offsets[:]),
                 )
-            codes = [keep.tile([P, HC], U32, name="codes%d%d" % (z, h), align_bytes=64) for h in range(HALVES)]
-            x_scales = [keep.tile([P, HC], U8, name="x_scales%d%d" % (z, h), align_bytes=64) for h in range(HALVES)]
-            for h in range(HALVES):
+            codes = keep.tile([P, S], U32, name="codes%d" % z, align_bytes=64)
+            x_scales = keep.tile([P, S], U8, name="x_scales%d" % z, align_bytes=64)
+            for q in range(QUARTERS):
+                cols = slice(q * QC, (q + 1) * QC)
                 nc.vector.quantize_mx(
-                    out=codes[h][:].bitcast(FP8X4),
-                    scales=x_scales[h][:],
-                    in_=picked[:, h].rearrange("p d v j -> p (d v j)"),
+                    out=codes[:, cols].bitcast(FP8X4),
+                    scales=x_scales[:, cols],
+                    in_=picked[:, q].rearrange("p d v j -> p (d v j)"),
                 )
-            for a in range(2):
-                for h in range(HALVES):
-                    nc.tensor.matmul_mx(
-                        out=banks[a][h][:],
-                        lhsT=w_words[a][:, z, :].bitcast(FP8X4),
-                        lhsT_scale=w_scales[:, a, z, :],
-                        rhs=codes[h][:].bitcast(FP8X4),
-                        rhs_scale=x_scales[h][:],
-                        start=(z == 0),
-                        stop=(z == PASSES - 1),
-                    )
+            for q in range(QUARTERS):
+                cols = slice(q * QC, (q + 1) * QC)
+                nc.tensor.matmul_mx(
+                    out=s_banks[q][:].rearrange("p d v -> p (d v)"),
+                    lhsT=w_words[0][:, z, :].bitcast(FP8X4),
+                    lhsT_scale=w_scales[:, 0, z, :],
+                    rhs=codes[:, cols].bitcast(FP8X4),
+                    rhs_scale=x_scales[:, cols],
+                    start=(z == 0),
+                    stop=(z == PASSES - 1),
+                )
+            for h in range(HALVES):
+                cols = slice(h * HC, (h + 1) * HC)
+                nc.tensor.matmul_mx(
+                    out=h_banks[h][:],
+                    lhsT=w_words[1][:, z, :].bitcast(FP8X4),
+                    lhsT_scale=w_scales[:, 1, z, :],
+                    rhs=codes[:, cols].bitcast(FP8X4),
+                    rhs_scale=x_scales[:, cols],
+                    start=(z == 0),
+                    stop=(z == PASSES - 1),
+                )
 
-        top = [keep.tile([P, VH], F32, name="top%d" % h) for h in range(HALVES)]
-        shifted = [keep.tile([P, D, VH], F32, name="shifted%d" % h) for h in range(HALVES)]
-        e = [keep.tile([P, D, VH], F32, name="e%d" % h) for h in range(HALVES)]
-        eh = [keep.tile([P, D, VH], F32, name="eh%d" % h) for h in range(HALVES)]
-        den = keep.tile([P, HALVES, VH], F32, name="den")
-        num = keep.tile([P, HALVES, VH], F32, name="num")
-        for h in range(HALVES):
-            nc.vector.tensor_reduce(out=top[h][:], in_=banks[0][h][:].rearrange("p (d v) -> p v d", d=D), axis=AX.X, op=ALU.max)
-        for h in range(HALVES):
+        top = keep.tile([P, QUARTERS, VQ], F32, name="top")
+        shifted = keep.tile([P, QUARTERS, D, VQ], F32, name="shifted")
+        e = keep.tile([P, QUARTERS, D, VQ], F32, name="e")
+        eh = keep.tile([P, QUARTERS, D, VQ], F32, name="eh")
+        for q in range(QUARTERS):
+            nc.vector.tensor_reduce(out=top[:, q, :], in_=s_banks[q][:].rearrange("p d v -> p v d"), axis=AX.X, op=ALU.max)
+        for q in range(QUARTERS):
             nc.vector.tensor_tensor(
-                out=shifted[h][:],
-                in0=banks[0][h][:].rearrange("p (d v) -> p d v", d=D),
-                in1=top[h][:].unsqueeze(1).to_broadcast([P, D, VH]),
+                out=shifted[:, q],
+                in0=s_banks[q][:],
+                in1=top[:, q, :].unsqueeze(1).to_broadcast([P, D, VQ]),
                 op=ALU.subtract,
             )
-            nc.scalar.activation(out=e[h][:], in_=shifted[h][:], func=ACT.Exp)
+            nc.scalar.activation(out=e[:, q], in_=shifted[:, q], func=ACT.Exp)
+        den = keep.tile([P, QUARTERS, VQ], F32, name="den")
         for h in range(HALVES):
-            nc.vector.tensor_reduce(out=den[:, h, :], in_=e[h][:].rearrange("p d v -> p v d"), axis=AX.X, op=ALU.add)
-            nc.vector.tensor_tensor(out=eh[h][:], in0=banks[1][h][:].rearrange("p (d v) -> p d v", d=D), in1=e[h][:], op=ALU.mult)
-        inv = keep.tile([P, V], F32, name="inv")
-        nc.vector.reciprocal(out=inv[:], in_=den[:].rearrange("p h v -> p (h v)"))
-        for h in range(HALVES):
-            nc.vector.tensor_reduce(out=num[:, h, :], in_=eh[h][:].rearrange("p d v -> p v d"), axis=AX.X, op=ALU.add)
+            qs = slice(2 * h, 2 * h + 2)
+            nc.vector.tensor_reduce(out=den[:, qs, :], in_=e[:, qs].rearrange("p q d v -> p q v d"), axis=AX.X, op=ALU.add)
+            nc.vector.tensor_tensor(
+                out=eh[:, qs].rearrange("p q d v -> p (q d v)"),
+                in0=h_banks[h][:],
+                in1=e[:, qs].rearrange("p q d v -> p (q d v)"),
+                op=ALU.mult,
+            )
+        den_halves = den[:].rearrange("p (h q) v -> p h (q v)", h=HALVES)
+        both = keep.tile([P, VH], F32, name="both")
+        nc.vector.tensor_tensor(out=both[:], in0=den_halves[:, 0, :], in1=den_halves[:, 1, :], op=ALU.mult)
+        num_pairs = keep.tile([P, QUARTERS, 2, VQ], F32, name="num_pairs")
+        nc.vector.tensor_tensor(out=num_pairs[:], in0=eh[:, :, 0:2, :], in1=eh[:, :, 2:4, :], op=ALU.add)
+        inv_both = keep.tile([P, VH], F32, name="inv_both")
+        nc.vector.reciprocal(out=inv_both[:], in_=both[:])
+        num = keep.tile([P, QUARTERS, VQ], F32, name="num")
+        nc.vector.tensor_tensor(out=num[:], in0=num_pairs[:, :, 0, :], in1=num_pairs[:, :, 1, :], op=ALU.add)
+        inv = keep.tile([P, HALVES, VH], F32, name="inv")
+        nc.vector.tensor_tensor(out=inv[:], in0=inv_both[:].unsqueeze(1).to_broadcast([P, HALVES, VH]), in1=den_halves[:, ::-1, :], op=ALU.mult)
         result = keep.tile([P, V], F32, name="result")
-        nc.vector.tensor_tensor(out=result[:], in0=num[:].rearrange("p h v -> p (h v)"), in1=inv[:], op=ALU.mult)
+        nc.vector.tensor_tensor(out=result[:], in0=num[:].rearrange("p q v -> p (q v)"), in1=inv[:].rearrange("p h v -> p (h v)"), op=ALU.mult)
         nc.sync.dma_start(out=out, in_=result[:])

@@ -26,6 +26,7 @@ QUARTERS = 4
 VQ = V // QUARTERS
 QC = D * VQ
 HC = D * VH
+LOADS = ((0, 0, 2), (0, 2, 2), (1, 0, 1), (1, 1, 1), (1, 2, 1), (1, 3, 1))
 
 
 def tile_picked_apool_none_e_kernel(tc, xT, w1_words, w1_scales, w2_words, w2_scales, offs, out):
@@ -35,47 +36,59 @@ def tile_picked_apool_none_e_kernel(tc, xT, w1_words, w1_scales, w2_words, w2_sc
         psum = ctx.enter_context(tc.psum_pool(name="psum", bufs=1))
 
         offsets = keep.tile([P, S // 16], U16, name="offsets")
-        planes = [keep.tile([P, T], F32, name="plane%d" % i, align_bytes=64) for i in range(PASSES * PACK)]
-        x_rows = xT.rearrange("(z p j) t -> z j p t", z=PASSES, j=PACK)
+        x_rows = xT.rearrange("(z p j) t -> z p j t", z=PASSES, j=PACK)
         w_words = [keep.tile([P, PASSES, N], I32, name="w_words%d" % i, align_bytes=64) for i in range(2)]
         w_scales = keep.tile([P, 2, PASSES, N], U8, name="w_scales", align_bytes=64)
 
         warm = keep.tile([P, 8], F32, name="warm")
         warm_out = keep.tile([P, 8], F32, name="warm_out")
+        nc.vector.memset(w_scales[:].rearrange("p a z n -> p (a z n)").bitcast(I32), 0)
         nc.vector.memset(warm[:], 0.0)
         nc.scalar.activation(out=warm_out[:], in_=warm[:], func=ACT.Exp)
 
-        nc.vector.memset(w_scales[:].rearrange("p a z n -> p (a z n)").bitcast(I32), 0)
-        for a, scales in enumerate((w1_scales, w2_scales)):
+        planes = []
+        for z, j0, count in LOADS:
+            rows = keep.tile([P, count, T], F32, name="rows%d%d" % (z, j0), align_bytes=64)
+            nc.sync.dma_start(out=rows[:], in_=x_rows[z, :, j0 : j0 + count, :])
+            planes.extend(rows[:, i, :] for i in range(count))
+            if len(planes) == count:
+                nc.sync.dma_start(offsets[:], offs)
+        for a, (words, scales) in enumerate(((w1_words, w1_scales), (w2_words, w2_scales))):
+            nc.sync.dma_start(out=w_words[a][:], in_=words.rearrange("z p n r -> p z (n r)").bitcast(I32))
             for q in range(4):
-                nc.scalar.dma_start(
+                nc.sync.dma_start(
                     out=w_scales[32 * q : 32 * q + 4, a, :, :].bitcast(I32),
                     in_=scales[:, 4 * q : 4 * q + 4, :].rearrange("z r n -> r z n").bitcast(I32),
                 )
 
-        for i in range(PASSES * PACK):
-            nc.sync.dma_start(out=planes[i][:], in_=x_rows[i // PACK, i % PACK])
-            if i == 0:
-                nc.sync.dma_start(offsets[:], offs)
-        for a, words in enumerate((w1_words, w2_words)):
-            nc.sync.dma_start(out=w_words[a][:], in_=words.rearrange("z p n r -> p z (n r)").bitcast(I32))
-
         s_banks = [psum.tile([P, D, VQ], F32, name="s_bank%d" % q) for q in range(QUARTERS)]
-        h_banks = [psum.tile([P, HC], F32, name="h_bank%d" % h) for h in range(HALVES)]
+        h_bank = psum.tile([P, S], F32, name="h_bank")
+        codes = []
+        x_scales = []
         for z in range(PASSES):
             picked = keep.tile([P, QUARTERS, D, VQ, PACK], BF16, name="picked%d" % z, align_bytes=64)
-            for j in range(PACK):
-                nc.vector.tensor_copy(
-                    out=picked[:, :, :, :, j].rearrange("p q d v -> p d q v"),
-                    in_=planes[PACK * z + j][:].indirect(offsets[:]),
-                )
-            codes = keep.tile([P, S], U32, name="codes%d" % z, align_bytes=64)
-            x_scales = keep.tile([P, S], U8, name="x_scales%d" % z, align_bytes=64)
+            for u in range(2):
+                if (z, u) == (PASSES - 1, 1):
+                    for j in (2, 3):
+                        nc.vector.tensor_copy(
+                            out=picked[:, :, :, :, j].rearrange("p q d v -> p d q v"),
+                            in_=planes[PACK * z + j].indirect(offsets[:]),
+                        )
+                else:
+                    dense = keep.tile([P, 2, S], F32, name="dense%d%d" % (z, u), align_bytes=64)
+                    for i in range(2):
+                        nc.vector.tensor_copy(out=dense[:, i, :], in_=planes[PACK * z + 2 * u + i].indirect(offsets[:]))
+                    nc.scalar.copy(
+                        out=picked[:, :, :, :, 2 * u : 2 * u + 2],
+                        in_=dense[:].rearrange("p i (d q v) -> p q d v i", d=D, q=QUARTERS),
+                    )
+            codes.append(keep.tile([P, S], U32, name="codes%d" % z, align_bytes=64))
+            x_scales.append(keep.tile([P, S], U8, name="x_scales%d" % z, align_bytes=64))
             for q in range(QUARTERS):
                 cols = slice(q * QC, (q + 1) * QC)
                 nc.vector.quantize_mx(
-                    out=codes[:, cols].bitcast(FP8X4),
-                    scales=x_scales[:, cols],
+                    out=codes[z][:, cols].bitcast(FP8X4),
+                    scales=x_scales[z][:, cols],
                     in_=picked[:, q].rearrange("p d v j -> p (d v j)"),
                 )
             for q in range(QUARTERS):
@@ -84,22 +97,21 @@ def tile_picked_apool_none_e_kernel(tc, xT, w1_words, w1_scales, w2_words, w2_sc
                     out=s_banks[q][:].rearrange("p d v -> p (d v)"),
                     lhsT=w_words[0][:, z, :].bitcast(FP8X4),
                     lhsT_scale=w_scales[:, 0, z, :],
-                    rhs=codes[:, cols].bitcast(FP8X4),
-                    rhs_scale=x_scales[:, cols],
+                    rhs=codes[z][:, cols].bitcast(FP8X4),
+                    rhs_scale=x_scales[z][:, cols],
                     start=(z == 0),
                     stop=(z == PASSES - 1),
                 )
-            for h in range(HALVES):
-                cols = slice(h * HC, (h + 1) * HC)
-                nc.tensor.matmul_mx(
-                    out=h_banks[h][:],
-                    lhsT=w_words[1][:, z, :].bitcast(FP8X4),
-                    lhsT_scale=w_scales[:, 1, z, :],
-                    rhs=codes[:, cols].bitcast(FP8X4),
-                    rhs_scale=x_scales[:, cols],
-                    start=(z == 0),
-                    stop=(z == PASSES - 1),
-                )
+        for z in reversed(range(PASSES)):
+            nc.tensor.matmul_mx(
+                out=h_bank[:],
+                lhsT=w_words[1][:, z, :].bitcast(FP8X4),
+                lhsT_scale=w_scales[:, 1, z, :],
+                rhs=codes[z][:].bitcast(FP8X4),
+                rhs_scale=x_scales[z][:],
+                start=(z == PASSES - 1),
+                stop=(z == 0),
+            )
 
         top = keep.tile([P, QUARTERS, VQ], F32, name="top")
         shifted = keep.tile([P, QUARTERS, D, VQ], F32, name="shifted")
@@ -119,23 +131,29 @@ def tile_picked_apool_none_e_kernel(tc, xT, w1_words, w1_scales, w2_words, w2_sc
         for h in range(HALVES):
             qs = slice(2 * h, 2 * h + 2)
             nc.vector.tensor_reduce(out=den[:, qs, :], in_=e[:, qs].rearrange("p q d v -> p q v d"), axis=AX.X, op=ALU.add)
+
+        def weigh(h):
+            qs = slice(2 * h, 2 * h + 2)
             nc.vector.tensor_tensor(
                 out=eh[:, qs].rearrange("p q d v -> p (q d v)"),
-                in0=h_banks[h][:],
+                in0=h_bank[:, h * HC : (h + 1) * HC],
                 in1=e[:, qs].rearrange("p q d v -> p (q d v)"),
                 op=ALU.mult,
             )
+
         den_halves = den[:].rearrange("p (h q) v -> p h (q v)", h=HALVES)
-        both = keep.tile([P, VH], F32, name="both")
-        nc.vector.tensor_tensor(out=both[:], in0=den_halves[:, 0, :], in1=den_halves[:, 1, :], op=ALU.mult)
+        both = e[:, 1, 0:2, :].rearrange("p d v -> p (d v)")
+        inv_both = e[:, 3, 0:2, :].rearrange("p d v -> p (d v)")
+        weigh(0)
+        nc.vector.tensor_tensor(out=both, in0=den_halves[:, 0, :], in1=den_halves[:, 1, :], op=ALU.mult)
+        weigh(1)
+        nc.vector.reciprocal(out=inv_both, in_=both)
         num_pairs = keep.tile([P, QUARTERS, 2, VQ], F32, name="num_pairs")
         nc.vector.tensor_tensor(out=num_pairs[:], in0=eh[:, :, 0:2, :], in1=eh[:, :, 2:4, :], op=ALU.add)
-        inv_both = keep.tile([P, VH], F32, name="inv_both")
-        nc.vector.reciprocal(out=inv_both[:], in_=both[:])
+        inv = keep.tile([P, HALVES, VH], F32, name="inv")
+        nc.vector.tensor_tensor(out=inv[:], in0=inv_both.unsqueeze(1).to_broadcast([P, HALVES, VH]), in1=den_halves[:, ::-1, :], op=ALU.mult)
         num = keep.tile([P, QUARTERS, VQ], F32, name="num")
         nc.vector.tensor_tensor(out=num[:], in0=num_pairs[:, :, 0, :], in1=num_pairs[:, :, 1, :], op=ALU.add)
-        inv = keep.tile([P, HALVES, VH], F32, name="inv")
-        nc.vector.tensor_tensor(out=inv[:], in0=inv_both[:].unsqueeze(1).to_broadcast([P, HALVES, VH]), in1=den_halves[:, ::-1, :], op=ALU.mult)
         result = keep.tile([P, V], F32, name="result")
         nc.vector.tensor_tensor(out=result[:], in0=num[:].rearrange("p q v -> p (q v)"), in1=inv[:].rearrange("p h v -> p (h v)"), op=ALU.mult)
         nc.sync.dma_start(out=out, in_=result[:])

@@ -26,7 +26,7 @@ QUARTERS = 4
 VQ = V // QUARTERS
 QC = D * VQ
 HC = D * VH
-LOADS = ((0, 0, 2), (0, 2, 2), (1, 0, 1), (1, 1, 1), (1, 2, 1), (1, 3, 1))
+LOADS = ((0, 0, 2), (0, 2, 1), (0, 3, 1), (1, 0, 1), (1, 1, 1), (1, 2, 1), (1, 3, 1))
 
 
 def tile_picked_apool_none_e_kernel(tc, xT, w1_words, w1_scales, w2_words, w2_scales, offs, out):
@@ -67,21 +67,11 @@ def tile_picked_apool_none_e_kernel(tc, xT, w1_words, w1_scales, w2_words, w2_sc
         x_scales = []
         for z in range(PASSES):
             picked = keep.tile([P, QUARTERS, D, VQ, PACK], BF16, name="picked%d" % z, align_bytes=64)
-            for u in range(2):
-                if (z, u) == (PASSES - 1, 1):
-                    for j in (2, 3):
-                        nc.vector.tensor_copy(
-                            out=picked[:, :, :, :, j].rearrange("p q d v -> p d q v"),
-                            in_=planes[PACK * z + j].indirect(offsets[:]),
-                        )
-                else:
-                    dense = keep.tile([P, 2, S], F32, name="dense%d%d" % (z, u), align_bytes=64)
-                    for i in range(2):
-                        nc.vector.tensor_copy(out=dense[:, i, :], in_=planes[PACK * z + 2 * u + i].indirect(offsets[:]))
-                    nc.scalar.copy(
-                        out=picked[:, :, :, :, 2 * u : 2 * u + 2],
-                        in_=dense[:].rearrange("p i (d q v) -> p q d v i", d=D, q=QUARTERS),
-                    )
+            for j in range(PACK):
+                nc.vector.tensor_copy(
+                    out=picked[:, :, :, :, j].rearrange("p q d v -> p d q v"),
+                    in_=planes[PACK * z + j].indirect(offsets[:]),
+                )
             codes.append(keep.tile([P, S], U32, name="codes%d" % z, align_bytes=64))
             x_scales.append(keep.tile([P, S], U8, name="x_scales%d" % z, align_bytes=64))
             for q in range(QUARTERS):

@@ -40,11 +40,7 @@ def tile_picked_apool_none_e_kernel(tc, xT, w1_words, w1_scales, w2_words, w2_sc
         w_words = [keep.tile([P, PASSES, N], I32, name="w_words%d" % i, align_bytes=64) for i in range(2)]
         w_scales = keep.tile([P, 2, PASSES, N], U8, name="w_scales", align_bytes=64)
 
-        warm = keep.tile([P, 8], F32, name="warm")
-        warm_out = keep.tile([P, 8], F32, name="warm_out")
         nc.vector.memset(w_scales[:].rearrange("p a z n -> p (a z n)").bitcast(I32), 0)
-        nc.vector.memset(warm[:], 0.0)
-        nc.scalar.activation(out=warm_out[:], in_=warm[:], func=ACT.Exp)
 
         planes = []
         for z, j0, count in LOADS:
@@ -56,13 +52,13 @@ def tile_picked_apool_none_e_kernel(tc, xT, w1_words, w1_scales, w2_words, w2_sc
         for a, (words, scales) in enumerate(((w1_words, w1_scales), (w2_words, w2_scales))):
             nc.sync.dma_start(out=w_words[a][:], in_=words.rearrange("z p n r -> p z (n r)").bitcast(I32))
             for q in range(4):
-                nc.sync.dma_start(
+                (nc.sync, nc.scalar)[a].dma_start(
                     out=w_scales[32 * q : 32 * q + 4, a, :, :].bitcast(I32),
                     in_=scales[:, 4 * q : 4 * q + 4, :].rearrange("z r n -> r z n").bitcast(I32),
                 )
 
         s_banks = [psum.tile([P, D, VQ], F32, name="s_bank%d" % q) for q in range(QUARTERS)]
-        h_bank = psum.tile([P, S], F32, name="h_bank")
+        h_banks = [psum.tile([P, HC], F32, name="h_bank%d" % h) for h in range(HALVES)]
         codes = []
         x_scales = []
         for z in range(PASSES):
@@ -92,21 +88,23 @@ def tile_picked_apool_none_e_kernel(tc, xT, w1_words, w1_scales, w2_words, w2_sc
                     start=(z == 0),
                     stop=(z == PASSES - 1),
                 )
-        for z in reversed(range(PASSES)):
-            nc.tensor.matmul_mx(
-                out=h_bank[:],
-                lhsT=w_words[1][:, z, :].bitcast(FP8X4),
-                lhsT_scale=w_scales[:, 1, z, :],
-                rhs=codes[z][:].bitcast(FP8X4),
-                rhs_scale=x_scales[z][:],
-                start=(z == PASSES - 1),
-                stop=(z == 0),
-            )
+        for h in range(HALVES):
+            cols = slice(h * HC, (h + 1) * HC)
+            for z in range(PASSES):
+                nc.tensor.matmul_mx(
+                    out=h_banks[h][:],
+                    lhsT=w_words[1][:, z, :].bitcast(FP8X4),
+                    lhsT_scale=w_scales[:, 1, z, :],
+                    rhs=codes[z][:, cols].bitcast(FP8X4),
+                    rhs_scale=x_scales[z][:, cols],
+                    start=(z == 0),
+                    stop=(z == PASSES - 1),
+                )
 
         top = keep.tile([P, QUARTERS, VQ], F32, name="top")
         shifted = keep.tile([P, QUARTERS, D, VQ], F32, name="shifted")
         e = keep.tile([P, QUARTERS, D, VQ], F32, name="e")
-        eh = keep.tile([P, QUARTERS, D, VQ], F32, name="eh")
+        eh = keep.tile([P, D, QUARTERS, VQ], F32, name="eh")
         for q in range(QUARTERS):
             nc.vector.tensor_reduce(out=top[:, q, :], in_=s_banks[q][:].rearrange("p d v -> p v d"), axis=AX.X, op=ALU.max)
         for q in range(QUARTERS):
@@ -118,32 +116,23 @@ def tile_picked_apool_none_e_kernel(tc, xT, w1_words, w1_scales, w2_words, w2_sc
             )
             nc.scalar.activation(out=e[:, q], in_=shifted[:, q], func=ACT.Exp)
         den = keep.tile([P, QUARTERS, VQ], F32, name="den")
+        inv = keep.tile([P, QUARTERS, VQ], F32, name="inv")
+        num_pairs = keep.tile([P, 2, QUARTERS, VQ], F32, name="num_pairs")
+        num = keep.tile([P, QUARTERS, VQ], F32, name="num")
         for h in range(HALVES):
             qs = slice(2 * h, 2 * h + 2)
-            nc.vector.tensor_reduce(out=den[:, qs, :], in_=e[:, qs].rearrange("p q d v -> p q v d"), axis=AX.X, op=ALU.add)
-
-        def weigh(h):
-            qs = slice(2 * h, 2 * h + 2)
             nc.vector.tensor_tensor(
-                out=eh[:, qs].rearrange("p q d v -> p (q d v)"),
-                in0=h_bank[:, h * HC : (h + 1) * HC],
-                in1=e[:, qs].rearrange("p q d v -> p (q d v)"),
+                out=eh[:, :, qs, :].rearrange("p d q v -> p q d v"),
+                in0=h_banks[h][:].rearrange("p (q d v) -> p q d v", d=D, v=VQ),
+                in1=e[:, qs],
                 op=ALU.mult,
             )
-
-        den_halves = den[:].rearrange("p (h q) v -> p h (q v)", h=HALVES)
-        both = e[:, 1, 0:2, :].rearrange("p d v -> p (d v)")
-        inv_both = e[:, 3, 0:2, :].rearrange("p d v -> p (d v)")
-        weigh(0)
-        nc.vector.tensor_tensor(out=both, in0=den_halves[:, 0, :], in1=den_halves[:, 1, :], op=ALU.mult)
-        weigh(1)
-        nc.vector.reciprocal(out=inv_both, in_=both)
-        num_pairs = keep.tile([P, QUARTERS, 2, VQ], F32, name="num_pairs")
-        nc.vector.tensor_tensor(out=num_pairs[:], in0=eh[:, :, 0:2, :], in1=eh[:, :, 2:4, :], op=ALU.add)
-        inv = keep.tile([P, HALVES, VH], F32, name="inv")
-        nc.vector.tensor_tensor(out=inv[:], in0=inv_both.unsqueeze(1).to_broadcast([P, HALVES, VH]), in1=den_halves[:, ::-1, :], op=ALU.mult)
-        num = keep.tile([P, QUARTERS, VQ], F32, name="num")
-        nc.vector.tensor_tensor(out=num[:], in0=num_pairs[:, :, 0, :], in1=num_pairs[:, :, 1, :], op=ALU.add)
+            nc.vector.tensor_reduce(out=den[:, qs, :], in_=e[:, qs].rearrange("p q d v -> p q v d"), axis=AX.X, op=ALU.add)
+            nc.gpsimd.tensor_tensor(out=num_pairs[:, :, qs, :], in0=eh[:, 0:2, qs, :], in1=eh[:, 2:4, qs, :], op=ALU.add)
+        nc.gpsimd.tensor_tensor(out=num[:], in0=num_pairs[:, 0], in1=num_pairs[:, 1], op=ALU.add)
+        for h in range(HALVES):
+            qs = slice(2 * h, 2 * h + 2)
+            nc.vector.reciprocal(out=inv[:, qs, :], in_=den[:, qs, :])
         result = keep.tile([P, V], F32, name="result")
-        nc.vector.tensor_tensor(out=result[:], in0=num[:].rearrange("p q v -> p (q v)"), in1=inv[:].rearrange("p h v -> p (h v)"), op=ALU.mult)
+        nc.vector.tensor_tensor(out=result[:], in0=num[:].rearrange("p q v -> p (q v)"), in1=inv[:].rearrange("p q v -> p (q v)"), op=ALU.mult)
         nc.sync.dma_start(out=out, in_=result[:])

@@ -102,37 +102,45 @@ def tile_picked_apool_none_e_kernel(tc, xT, w1_words, w1_scales, w2_words, w2_sc
                 )
 
         top = keep.tile([P, QUARTERS, VQ], F32, name="top")
-        shifted = keep.tile([P, QUARTERS, D, VQ], F32, name="shifted")
-        e = keep.tile([P, QUARTERS, D, VQ], F32, name="e")
-        eh = keep.tile([P, D, QUARTERS, VQ], F32, name="eh")
+        shifted = keep.tile([P, QUARTERS, VQ, D], F32, name="shifted")
+        e = keep.tile([P, QUARTERS, VQ, D], F32, name="e")
+        eh = keep.tile([P, QUARTERS, VQ, D], F32, name="eh")
         for q in range(QUARTERS):
             nc.vector.tensor_reduce(out=top[:, q, :], in_=s_banks[q][:].rearrange("p d v -> p v d"), axis=AX.X, op=ALU.max)
         for q in range(QUARTERS):
             nc.vector.tensor_tensor(
                 out=shifted[:, q],
-                in0=s_banks[q][:],
-                in1=top[:, q, :].unsqueeze(1).to_broadcast([P, D, VQ]),
+                in0=s_banks[q][:].rearrange("p d v -> p v d"),
+                in1=top[:, q, :].unsqueeze(2).to_broadcast([P, VQ, D]),
                 op=ALU.subtract,
             )
             nc.scalar.activation(out=e[:, q], in_=shifted[:, q], func=ACT.Exp)
         den = keep.tile([P, QUARTERS, VQ], F32, name="den")
         inv = keep.tile([P, QUARTERS, VQ], F32, name="inv")
-        num_pairs = keep.tile([P, 2, QUARTERS, VQ], F32, name="num_pairs")
-        num = keep.tile([P, QUARTERS, VQ], F32, name="num")
+        num_pairs = keep.tile([P, V, 2], F32, name="num_pairs")
+        num = keep.tile([P, V], F32, name="num")
         for h in range(HALVES):
             qs = slice(2 * h, 2 * h + 2)
             nc.vector.tensor_tensor(
-                out=eh[:, :, qs, :].rearrange("p d q v -> p q d v"),
-                in0=h_banks[h][:].rearrange("p (q d v) -> p q d v", d=D, v=VQ),
+                out=eh[:, qs],
+                in0=h_banks[h][:].rearrange("p (q d v) -> p q v d", d=D, v=VQ),
                 in1=e[:, qs],
                 op=ALU.mult,
             )
-            nc.vector.tensor_reduce(out=den[:, qs, :], in_=e[:, qs].rearrange("p q d v -> p q v d"), axis=AX.X, op=ALU.add)
-            nc.gpsimd.tensor_tensor(out=num_pairs[:, :, qs, :], in0=eh[:, 0:2, qs, :], in1=eh[:, 2:4, qs, :], op=ALU.add)
-        nc.gpsimd.tensor_tensor(out=num[:], in0=num_pairs[:, 0], in1=num_pairs[:, 1], op=ALU.add)
+            neighbours = eh[:, qs].rearrange("p q v (a b) -> p (q v a) b", b=2)
+            nc.gpsimd.tensor_tensor(
+                out=num_pairs[:, h * VH : (h + 1) * VH, :].rearrange("p v a -> p (v a)"),
+                in0=neighbours[:, :, 0],
+                in1=neighbours[:, :, 1],
+                op=ALU.add,
+            )
+        nc.gpsimd.tensor_tensor(out=num[:], in0=num_pairs[:, :, 0], in1=num_pairs[:, :, 1], op=ALU.add)
+        for h in range(HALVES):
+            qs = slice(2 * h, 2 * h + 2)
+            nc.vector.tensor_reduce(out=den[:, qs, :], in_=e[:, qs], axis=AX.X, op=ALU.add)
         for h in range(HALVES):
             qs = slice(2 * h, 2 * h + 2)
             nc.vector.reciprocal(out=inv[:, qs, :], in_=den[:, qs, :])
         result = keep.tile([P, V], F32, name="result")
-        nc.vector.tensor_tensor(out=result[:], in0=num[:].rearrange("p q v -> p (q v)"), in1=inv[:].rearrange("p q v -> p (q v)"), op=ALU.mult)
+        nc.vector.tensor_tensor(out=result[:], in0=num[:], in1=inv[:].rearrange("p q v -> p (q v)"), op=ALU.mult)
         nc.sync.dma_start(out=out, in_=result[:])

@@ -37,7 +37,7 @@ def tile_picked_apool_none_e_kernel(tc, xT, w1_words, w1_scales, w2_words, w2_sc
 
         offsets = keep.tile([P, S // 16], U16, name="offsets")
         x_rows = xT.rearrange("(z p j) t -> z p j t", z=PASSES, j=PACK)
-        w_words = [keep.tile([P, PASSES, N], I32, name="w_words%d" % i, align_bytes=64) for i in range(2)]
+        w_words = [[keep.tile([P, N], I32, name="w_words%d%d" % (a, z), align_bytes=64) for z in range(PASSES)] for a in range(2)]
         w_scales = keep.tile([P, 2, PASSES, N], U8, name="w_scales", align_bytes=64)
 
         nc.vector.memset(w_scales[:].rearrange("p a z n -> p (a z n)").bitcast(I32), 0)
@@ -49,10 +49,12 @@ def tile_picked_apool_none_e_kernel(tc, xT, w1_words, w1_scales, w2_words, w2_sc
             planes.extend(rows[:, i, :] for i in range(count))
             if len(planes) == count:
                 nc.sync.dma_start(offsets[:], offs)
-        for a, (words, scales) in enumerate(((w1_words, w1_scales), (w2_words, w2_scales))):
-            nc.sync.dma_start(out=w_words[a][:], in_=words.rearrange("z p n r -> p z (n r)").bitcast(I32))
+        for z in range(PASSES):
+            for a, words in enumerate((w1_words, w2_words)):
+                nc.sync.dma_start(out=w_words[a][z][:], in_=words[z].rearrange("p n r -> p (n r)").bitcast(I32))
+        for a, scales in enumerate((w1_scales, w2_scales)):
             for q in range(4):
-                (nc.sync, nc.scalar)[a].dma_start(
+                nc.gpsimd.dma_start(
                     out=w_scales[32 * q : 32 * q + 4, a, :, :].bitcast(I32),
                     in_=scales[:, 4 * q : 4 * q + 4, :].rearrange("z r n -> r z n").bitcast(I32),
                 )
@@ -81,19 +83,18 @@ def tile_picked_apool_none_e_kernel(tc, xT, w1_words, w1_scales, w2_words, w2_sc
                 cols = slice(q * QC, (q + 1) * QC)
                 nc.tensor.matmul_mx(
                     out=s_banks[q][:].rearrange("p d v -> p (d v)"),
-                    lhsT=w_words[0][:, z, :].bitcast(FP8X4),
+                    lhsT=w_words[0][z][:].bitcast(FP8X4),
                     lhsT_scale=w_scales[:, 0, z, :],
                     rhs=codes[z][:, cols].bitcast(FP8X4),
                     rhs_scale=x_scales[z][:, cols],
                     start=(z == 0),
                     stop=(z == PASSES - 1),
                 )
-        for h in range(HALVES):
-            cols = slice(h * HC, (h + 1) * HC)
-            for z in range(PASSES):
+            for h in range(HALVES):
+                cols = slice(h * HC, (h + 1) * HC)
                 nc.tensor.matmul_mx(
                     out=h_banks[h][:],
-                    lhsT=w_words[1][:, z, :].bitcast(FP8X4),
+                    lhsT=w_words[1][z][:].bitcast(FP8X4),
                     lhsT_scale=w_scales[:, 1, z, :],
                     rhs=codes[z][:, cols].bitcast(FP8X4),
                     rhs_scale=x_scales[z][:, cols],
@@ -105,16 +106,18 @@ def tile_picked_apool_none_e_kernel(tc, xT, w1_words, w1_scales, w2_words, w2_sc
         shifted = keep.tile([P, QUARTERS, VQ, D], F32, name="shifted")
         e = keep.tile([P, QUARTERS, VQ, D], F32, name="e")
         eh = keep.tile([P, QUARTERS, VQ, D], F32, name="eh")
-        for q in range(QUARTERS):
-            nc.vector.tensor_reduce(out=top[:, q, :], in_=s_banks[q][:].rearrange("p d v -> p v d"), axis=AX.X, op=ALU.max)
-        for q in range(QUARTERS):
-            nc.vector.tensor_tensor(
-                out=shifted[:, q],
-                in0=s_banks[q][:].rearrange("p d v -> p v d"),
-                in1=top[:, q, :].unsqueeze(2).to_broadcast([P, VQ, D]),
-                op=ALU.subtract,
-            )
-            nc.scalar.activation(out=e[:, q], in_=shifted[:, q], func=ACT.Exp)
+        for step in range(QUARTERS + 1):
+            if step < QUARTERS:
+                nc.vector.tensor_reduce(out=top[:, step, :], in_=s_banks[step][:].rearrange("p d v -> p v d"), axis=AX.X, op=ALU.max)
+            if step > 0:
+                q = step - 1
+                nc.vector.tensor_tensor(
+                    out=shifted[:, q],
+                    in0=s_banks[q][:].rearrange("p d v -> p v d"),
+                    in1=top[:, q, :].unsqueeze(2).to_broadcast([P, VQ, D]),
+                    op=ALU.subtract,
+                )
+                nc.scalar.activation(out=e[:, q], in_=shifted[:, q], func=ACT.Exp)
         den = keep.tile([P, QUARTERS, VQ], F32, name="den")
         inv = keep.tile([P, QUARTERS, VQ], F32, name="inv")
         num_pairs = keep.tile([P, V, 2], F32, name="num_pairs")

@@ -26,6 +26,7 @@ QUARTERS = 4
 VQ = V // QUARTERS
 QC = D * VQ
 HC = D * VH
+LAG = 2
 LOADS = ((0, 0, 2), (0, 2, 1), (0, 3, 1), (1, 0, 1), (1, 1, 1), (1, 2, 1), (1, 3, 1))
 
 
@@ -106,41 +107,46 @@ def tile_picked_apool_none_e_kernel(tc, xT, w1_words, w1_scales, w2_words, w2_sc
         shifted = keep.tile([P, QUARTERS, VQ, D], F32, name="shifted")
         e = keep.tile([P, QUARTERS, VQ, D], F32, name="e")
         eh = keep.tile([P, QUARTERS, VQ, D], F32, name="eh")
-        for step in range(QUARTERS + 1):
+        def take_max(q):
+            nc.vector.tensor_reduce(out=top[:, q, :], in_=s_banks[q][:].rearrange("p d v -> p v d"), axis=AX.X, op=ALU.max)
+
+        def take_exp(q):
+            nc.vector.tensor_tensor(
+                out=shifted[:, q],
+                in0=s_banks[q][:].rearrange("p d v -> p v d"),
+                in1=top[:, q, :].unsqueeze(2).to_broadcast([P, VQ, D]),
+                op=ALU.subtract,
+            )
+            nc.scalar.activation(out=e[:, q], in_=shifted[:, q], func=ACT.Exp)
+
+        for step in range(QUARTERS + LAG):
             if step < QUARTERS:
-                nc.vector.tensor_reduce(out=top[:, step, :], in_=s_banks[step][:].rearrange("p d v -> p v d"), axis=AX.X, op=ALU.max)
-            if step > 0:
-                q = step - 1
-                nc.vector.tensor_tensor(
-                    out=shifted[:, q],
-                    in0=s_banks[q][:].rearrange("p d v -> p v d"),
-                    in1=top[:, q, :].unsqueeze(2).to_broadcast([P, VQ, D]),
-                    op=ALU.subtract,
-                )
-                nc.scalar.activation(out=e[:, q], in_=shifted[:, q], func=ACT.Exp)
+                take_max(step)
+            if step >= LAG:
+                take_exp(step - LAG)
         den = keep.tile([P, QUARTERS, VQ], F32, name="den")
         inv = keep.tile([P, QUARTERS, VQ], F32, name="inv")
         num_pairs = keep.tile([P, V, 2], F32, name="num_pairs")
         num = keep.tile([P, V], F32, name="num")
-        for h in range(HALVES):
-            qs = slice(2 * h, 2 * h + 2)
+        for q0, q1 in ((0, 1), (1, 2), (2, 4)):
+            h = q0 // 2
+            qs = slice(q0, q1)
             nc.vector.tensor_tensor(
                 out=eh[:, qs],
-                in0=h_banks[h][:].rearrange("p (q d v) -> p q v d", d=D, v=VQ),
+                in0=h_banks[h][:].rearrange("p (q d v) -> p q v d", d=D, v=VQ)[:, q0 - 2 * h : q1 - 2 * h],
                 in1=e[:, qs],
                 op=ALU.mult,
             )
-            neighbours = eh[:, qs].rearrange("p q v (a b) -> p (q v a) b", b=2)
-            nc.gpsimd.tensor_tensor(
-                out=num_pairs[:, h * VH : (h + 1) * VH, :].rearrange("p v a -> p (v a)"),
-                in0=neighbours[:, :, 0],
-                in1=neighbours[:, :, 1],
-                op=ALU.add,
-            )
-        nc.gpsimd.tensor_tensor(out=num[:], in0=num_pairs[:, :, 0], in1=num_pairs[:, :, 1], op=ALU.add)
-        for h in range(HALVES):
-            qs = slice(2 * h, 2 * h + 2)
             nc.vector.tensor_reduce(out=den[:, qs, :], in_=e[:, qs], axis=AX.X, op=ALU.add)
+            if q1 % 2 == 0:
+                neighbours = eh[:, 2 * h : 2 * h + 2].rearrange("p q v (a b) -> p (q v a) b", b=2)
+                nc.gpsimd.tensor_tensor(
+                    out=num_pairs[:, h * VH : (h + 1) * VH, :].rearrange("p v a -> p (v a)"),
+                    in0=neighbours[:, :, 0],
+                    in1=neighbours[:, :, 1],
+                    op=ALU.add,
+                )
+        nc.gpsimd.tensor_tensor(out=num[:], in0=num_pairs[:, :, 0], in1=num_pairs[:, :, 1], op=ALU.add)
         for h in range(HALVES):
             qs = slice(2 * h, 2 * h + 2)
             nc.vector.reciprocal(out=inv[:, qs, :], in_=den[:, qs, :])

@@ -106,7 +106,7 @@ def tile_picked_apool_none_e_kernel(tc, xT, w1_words, w1_scales, w2_words, w2_sc
         top = keep.tile([P, QUARTERS, VQ], F32, name="top")
         shifted = keep.tile([P, QUARTERS, VQ, D], F32, name="shifted")
         e = keep.tile([P, QUARTERS, VQ, D], F32, name="e")
-        eh = keep.tile([P, QUARTERS, VQ, D], F32, name="eh")
+        eh = keep.tile([P, D, QUARTERS, VQ], F32, name="eh")
         def take_max(q):
             nc.vector.tensor_reduce(out=top[:, q, :], in_=s_banks[q][:].rearrange("p d v -> p v d"), axis=AX.X, op=ALU.max)
 
@@ -126,27 +126,22 @@ def tile_picked_apool_none_e_kernel(tc, xT, w1_words, w1_scales, w2_words, w2_sc
                 take_exp(step - LAG)
         den = keep.tile([P, QUARTERS, VQ], F32, name="den")
         inv = keep.tile([P, QUARTERS, VQ], F32, name="inv")
-        num_pairs = keep.tile([P, V, 2], F32, name="num_pairs")
+        num_pairs = keep.tile([P, 2, QUARTERS, VQ], F32, name="num_pairs")
         num = keep.tile([P, V], F32, name="num")
         for q0, q1 in ((0, 1), (1, 2), (2, 4)):
             h = q0 // 2
             qs = slice(q0, q1)
             nc.vector.tensor_tensor(
-                out=eh[:, qs],
+                out=eh[:, :, qs, :].rearrange("p d q v -> p q v d"),
                 in0=h_banks[h][:].rearrange("p (q d v) -> p q v d", d=D, v=VQ)[:, q0 - 2 * h : q1 - 2 * h],
                 in1=e[:, qs],
                 op=ALU.mult,
             )
             nc.vector.tensor_reduce(out=den[:, qs, :], in_=e[:, qs], axis=AX.X, op=ALU.add)
             if q1 % 2 == 0:
-                neighbours = eh[:, 2 * h : 2 * h + 2].rearrange("p q v (a b) -> p (q v a) b", b=2)
-                nc.gpsimd.tensor_tensor(
-                    out=num_pairs[:, h * VH : (h + 1) * VH, :].rearrange("p v a -> p (v a)"),
-                    in0=neighbours[:, :, 0],
-                    in1=neighbours[:, :, 1],
-                    op=ALU.add,
-                )
-        nc.gpsimd.tensor_tensor(out=num[:], in0=num_pairs[:, :, 0], in1=num_pairs[:, :, 1], op=ALU.add)
+                half = slice(2 * h, 2 * h + 2)
+                nc.gpsimd.tensor_tensor(out=num_pairs[:, :, half, :], in0=eh[:, 0:2, half, :], in1=eh[:, 2:4, half, :], op=ALU.add)
+        nc.gpsimd.tensor_tensor(out=num[:], in0=num_pairs[:, 0].rearrange("p q v -> p (q v)"), in1=num_pairs[:, 1].rearrange("p q v -> p (q v)"), op=ALU.add)
         for h in range(HALVES):
             qs = slice(2 * h, 2 * h + 2)
             nc.vector.reciprocal(out=inv[:, qs, :], in_=den[:, qs, :])

@@ -39,9 +39,18 @@ def tile_picked_apool_none_e_kernel(tc, xT, w1_words, w1_scales, w2_words, w2_sc
         offsets = keep.tile([P, S // 16], U16, name="offsets")
         x_rows = xT.rearrange("(z p j) t -> z p j t", z=PASSES, j=PACK)
         w_words = [[keep.tile([P, N], I32, name="w_words%d%d" % (a, z), align_bytes=64) for z in range(PASSES)] for a in range(2)]
-        w_scales = keep.tile([P, 2, PASSES, N], U8, name="w_scales", align_bytes=64)
+        w_scales = [keep.tile([P, PASSES, N], U8, name="w_scales%d" % a, align_bytes=64) for a in range(2)]
+        staged = keep.tile([P, PASSES, N // 4], I32, name="staged")
 
-        nc.vector.memset(w_scales[:].rearrange("p a z n -> p (a z n)").bitcast(I32), 0)
+        def scale_rows(scales, q):
+            return scales[:, 4 * q : 4 * q + 4, :].rearrange("z r n -> r z n").bitcast(I32)
+
+        for q in range(4):
+            nc.scalar.dma_start(out=staged[32 * q : 32 * q + 4], in_=scale_rows(w1_scales, q))
+        for a in range(2):
+            nc.gpsimd.memset(w_scales[a][:].rearrange("p z n -> p (z n)").bitcast(I32), 0)
+        for q in range(4):
+            nc.gpsimd.tensor_copy(out=w_scales[0][32 * q : 32 * q + 4].bitcast(I32), in_=staged[32 * q : 32 * q + 4])
 
         planes = []
         for z, j0, count in LOADS:
@@ -50,15 +59,11 @@ def tile_picked_apool_none_e_kernel(tc, xT, w1_words, w1_scales, w2_words, w2_sc
             planes.extend(rows[:, i, :] for i in range(count))
             if len(planes) == count:
                 nc.sync.dma_start(offsets[:], offs)
+        for q in range(4):
+            nc.sync.dma_start(out=w_scales[1][32 * q : 32 * q + 4].bitcast(I32), in_=scale_rows(w2_scales, q))
         for z in range(PASSES):
             for a, words in enumerate((w1_words, w2_words)):
                 nc.sync.dma_start(out=w_words[a][z][:], in_=words[z].rearrange("p n r -> p (n r)").bitcast(I32))
-        for a, scales in enumerate((w1_scales, w2_scales)):
-            for q in range(4):
-                nc.gpsimd.dma_start(
-                    out=w_scales[32 * q : 32 * q + 4, a, :, :].bitcast(I32),
-                    in_=scales[:, 4 * q : 4 * q + 4, :].rearrange("z r n -> r z n").bitcast(I32),
-                )
 
         s_banks = [psum.tile([P, D, VQ], F32, name="s_bank%d" % q) for q in range(QUARTERS)]
         h_banks = [psum.tile([P, HC], F32, name="h_bank%d" % h) for h in range(HALVES)]
@@ -85,7 +90,7 @@ def tile_picked_apool_none_e_kernel(tc, xT, w1_words, w1_scales, w2_words, w2_sc
                 nc.tensor.matmul_mx(
                     out=s_banks[q][:].rearrange("p d v -> p (d v)"),
                     lhsT=w_words[0][z][:].bitcast(FP8X4),
-                    lhsT_scale=w_scales[:, 0, z, :],
+                    lhsT_scale=w_scales[0][:, z, :],
                     rhs=codes[z][:, cols].bitcast(FP8X4),
                     rhs_scale=x_scales[z][:, cols],
                     start=(z == 0),
@@ -96,7 +101,7 @@ def tile_picked_apool_none_e_kernel(tc, xT, w1_words, w1_scales, w2_words, w2_sc
                 nc.tensor.matmul_mx(
                     out=h_banks[h][:],
                     lhsT=w_words[1][z][:].bitcast(FP8X4),
-                    lhsT_scale=w_scales[:, 1, z, :],
+                    lhsT_scale=w_scales[1][:, z, :],
                     rhs=codes[z][:, cols].bitcast(FP8X4),
                     rhs_scale=x_scales[z][:, cols],
                     start=(z == 0),

@@ -20,14 +20,15 @@ P = 128
 PACK = 4
 PASSES = K // (P * PACK)
 D = S // V
-HALVES = 2
-VH = V // HALVES
+GROUPS = 4
+SCALE_ROWS = 4
 QUARTERS = 4
 VQ = V // QUARTERS
 QC = D * VQ
-HC = D * VH
+HALVES = 2
+HC = S // HALVES
+FIRST_LOAD_PLANES = 2
 LAG = 2
-LOADS = ((0, 0, 2), (0, 2, 1), (0, 3, 1), (1, 0, 1), (1, 1, 1), (1, 2, 1), (1, 3, 1))
 
 
 def tile_picked_apool_none_e_kernel(tc, xT, w1_words, w1_scales, w2_words, w2_scales, offs, out):
@@ -42,33 +43,36 @@ def tile_picked_apool_none_e_kernel(tc, xT, w1_words, w1_scales, w2_words, w2_sc
         w_scales = [keep.tile([P, PASSES, N], U8, name="w_scales%d" % a, align_bytes=64) for a in range(2)]
         staged = keep.tile([P, PASSES, N // 4], I32, name="staged")
 
-        def scale_rows(scales, q):
-            return scales[:, 4 * q : 4 * q + 4, :].rearrange("z r n -> r z n").bitcast(I32)
+        def live(g):
+            return slice(32 * g, 32 * g + SCALE_ROWS)
 
-        for q in range(4):
-            nc.scalar.dma_start(out=staged[32 * q : 32 * q + 4], in_=scale_rows(w1_scales, q))
+        def scale_rows(scales, g):
+            return scales[:, SCALE_ROWS * g : SCALE_ROWS * (g + 1), :].rearrange("z r n -> r z n").bitcast(I32)
+
+        for g in range(GROUPS):
+            nc.scalar.dma_start(out=staged[live(g)], in_=scale_rows(w1_scales, g))
         for a in range(2):
             nc.gpsimd.memset(w_scales[a][:].rearrange("p z n -> p (z n)").bitcast(I32), 0)
-        for q in range(4):
-            nc.gpsimd.tensor_copy(out=w_scales[0][32 * q : 32 * q + 4].bitcast(I32), in_=staged[32 * q : 32 * q + 4])
+        for g in range(GROUPS):
+            nc.gpsimd.tensor_copy(out=w_scales[0][live(g)].bitcast(I32), in_=staged[live(g)])
 
         planes = []
-        for z, j0, count in LOADS:
+        while len(planes) < PASSES * PACK:
+            z, j0 = divmod(len(planes), PACK)
+            count = FIRST_LOAD_PLANES if not planes else 1
             rows = keep.tile([P, count, T], F32, name="rows%d%d" % (z, j0), align_bytes=64)
             nc.sync.dma_start(out=rows[:], in_=x_rows[z, :, j0 : j0 + count, :])
-            planes.extend(rows[:, i, :] for i in range(count))
-            if len(planes) == count:
+            if not planes:
                 nc.sync.dma_start(offsets[:], offs)
-        for q in range(4):
-            nc.sync.dma_start(out=w_scales[1][32 * q : 32 * q + 4].bitcast(I32), in_=scale_rows(w2_scales, q))
+            planes.extend(rows[:, i, :] for i in range(count))
+        for g in range(GROUPS):
+            nc.sync.dma_start(out=w_scales[1][live(g)].bitcast(I32), in_=scale_rows(w2_scales, g))
         for z in range(PASSES):
             for a, words in enumerate((w1_words, w2_words)):
                 nc.sync.dma_start(out=w_words[a][z][:], in_=words[z].rearrange("p n r -> p (n r)").bitcast(I32))
 
         s_banks = [psum.tile([P, D, VQ], F32, name="s_bank%d" % q) for q in range(QUARTERS)]
         h_banks = [psum.tile([P, HC], F32, name="h_bank%d" % h) for h in range(HALVES)]
-        codes = []
-        x_scales = []
         for z in range(PASSES):
             picked = keep.tile([P, QUARTERS, D, VQ, PACK], BF16, name="picked%d" % z, align_bytes=64)
             for j in range(PACK):
@@ -76,13 +80,13 @@ def tile_picked_apool_none_e_kernel(tc, xT, w1_words, w1_scales, w2_words, w2_sc
                     out=picked[:, :, :, :, j].rearrange("p q d v -> p d q v"),
                     in_=planes[PACK * z + j].indirect(offsets[:]),
                 )
-            codes.append(keep.tile([P, S], U32, name="codes%d" % z, align_bytes=64))
-            x_scales.append(keep.tile([P, S], U8, name="x_scales%d" % z, align_bytes=64))
+            codes = keep.tile([P, S], U32, name="codes%d" % z, align_bytes=64)
+            x_scales = keep.tile([P, S], U8, name="x_scales%d" % z, align_bytes=64)
             for q in range(QUARTERS):
                 cols = slice(q * QC, (q + 1) * QC)
                 nc.vector.quantize_mx(
-                    out=codes[z][:, cols].bitcast(FP8X4),
-                    scales=x_scales[z][:, cols],
+                    out=codes[:, cols].bitcast(FP8X4),
+                    scales=x_scales[:, cols],
                     in_=picked[:, q].rearrange("p d v j -> p (d v j)"),
                 )
             for q in range(QUARTERS):
@@ -91,8 +95,8 @@ def tile_picked_apool_none_e_kernel(tc, xT, w1_words, w1_scales, w2_words, w2_sc
                     out=s_banks[q][:].rearrange("p d v -> p (d v)"),
                     lhsT=w_words[0][z][:].bitcast(FP8X4),
                     lhsT_scale=w_scales[0][:, z, :],
-                    rhs=codes[z][:, cols].bitcast(FP8X4),
-                    rhs_scale=x_scales[z][:, cols],
+                    rhs=codes[:, cols].bitcast(FP8X4),
+                    rhs_scale=x_scales[:, cols],
                     start=(z == 0),
                     stop=(z == PASSES - 1),
                 )
@@ -102,8 +106,8 @@ def tile_picked_apool_none_e_kernel(tc, xT, w1_words, w1_scales, w2_words, w2_sc
                     out=h_banks[h][:],
                     lhsT=w_words[1][z][:].bitcast(FP8X4),
                     lhsT_scale=w_scales[1][:, z, :],
-                    rhs=codes[z][:, cols].bitcast(FP8X4),
-                    rhs_scale=x_scales[z][:, cols],
+                    rhs=codes[:, cols].bitcast(FP8X4),
+                    rhs_scale=x_scales[:, cols],
                     start=(z == 0),
                     stop=(z == PASSES - 1),
                 )
@@ -112,43 +116,37 @@ def tile_picked_apool_none_e_kernel(tc, xT, w1_words, w1_scales, w2_words, w2_sc
         shifted = keep.tile([P, QUARTERS, VQ, D], F32, name="shifted")
         e = keep.tile([P, QUARTERS, VQ, D], F32, name="e")
         eh = keep.tile([P, D, QUARTERS, VQ], F32, name="eh")
-        def take_max(q):
-            nc.vector.tensor_reduce(out=top[:, q, :], in_=s_banks[q][:].rearrange("p d v -> p v d"), axis=AX.X, op=ALU.max)
-
-        def take_exp(q):
-            nc.vector.tensor_tensor(
-                out=shifted[:, q],
-                in0=s_banks[q][:].rearrange("p d v -> p v d"),
-                in1=top[:, q, :].unsqueeze(2).to_broadcast([P, VQ, D]),
-                op=ALU.subtract,
-            )
-            nc.scalar.activation(out=e[:, q], in_=shifted[:, q], func=ACT.Exp)
-
         for step in range(QUARTERS + LAG):
             if step < QUARTERS:
-                take_max(step)
+                nc.vector.tensor_reduce(out=top[:, step, :], in_=s_banks[step][:].rearrange("p d v -> p v d"), axis=AX.X, op=ALU.max)
             if step >= LAG:
-                take_exp(step - LAG)
+                q = step - LAG
+                nc.vector.tensor_tensor(
+                    out=shifted[:, q],
+                    in0=s_banks[q][:].rearrange("p d v -> p v d"),
+                    in1=top[:, q, :].unsqueeze(2).to_broadcast([P, VQ, D]),
+                    op=ALU.subtract,
+                )
+                nc.scalar.activation(out=e[:, q], in_=shifted[:, q], func=ACT.Exp)
+
         den = keep.tile([P, QUARTERS, VQ], F32, name="den")
         inv = keep.tile([P, QUARTERS, VQ], F32, name="inv")
         num_pairs = keep.tile([P, 2, QUARTERS, VQ], F32, name="num_pairs")
         num = keep.tile([P, V], F32, name="num")
-        for q0, q1 in ((0, 1), (1, 2), (2, 4)):
-            h = q0 // 2
-            qs = slice(q0, q1)
-            nc.vector.tensor_tensor(
-                out=eh[:, :, qs, :].rearrange("p d q v -> p q v d"),
-                in0=h_banks[h][:].rearrange("p (q d v) -> p q v d", d=D, v=VQ)[:, q0 - 2 * h : q1 - 2 * h],
-                in1=e[:, qs],
-                op=ALU.mult,
-            )
+        stretches = (slice(0, 1), slice(1, QUARTERS))
+        for qs in stretches:
+            for q in range(qs.start, qs.stop):
+                h, q_in_half = divmod(q, QUARTERS // HALVES)
+                nc.vector.tensor_tensor(
+                    out=eh[:, :, q, :].rearrange("p d v -> p v d"),
+                    in0=h_banks[h][:].rearrange("p (q d v) -> p q v d", d=D, v=VQ)[:, q_in_half],
+                    in1=e[:, q],
+                    op=ALU.mult,
+                )
+            nc.gpsimd.tensor_tensor(out=num_pairs[:, :, qs, :], in0=eh[:, 0:2, qs, :], in1=eh[:, 2:4, qs, :], op=ALU.add)
             nc.vector.tensor_reduce(out=den[:, qs, :], in_=e[:, qs], axis=AX.X, op=ALU.add)
-            if q1 % 2 == 0:
-                half = slice(2 * h, 2 * h + 2)
-                nc.gpsimd.tensor_tensor(out=num_pairs[:, :, half, :], in0=eh[:, 0:2, half, :], in1=eh[:, 2:4, half, :], op=ALU.add)
         nc.gpsimd.tensor_tensor(out=num[:], in0=num_pairs[:, 0].rearrange("p q v -> p (q v)"), in1=num_pairs[:, 1].rearrange("p q v -> p (q v)"), op=ALU.add)
-        for h in range(HALVES):
-            qs = slice(2 * h, 2 * h + 2)
+        for qs in stretches:
             nc.vector.reciprocal(out=inv[:, qs, :], in_=den[:, qs, :])
         result = keep.tile([P, V], F32, name="result")
         nc.vector.tensor_tensor(out=result[:], in0=num[:], in1=inv[:].rearrange("p q v -> p (q v)"), op=ALU.mult)

@@ -76,10 +76,16 @@ def tile_picked_apool_none_e_kernel(tc, xT, w1_words, w1_scales, w2_words, w2_sc
         for z in range(PASSES):
             picked = keep.tile([P, QUARTERS, D, VQ, PACK], BF16, name="picked%d" % z, align_bytes=64)
             for j in range(PACK):
-                nc.vector.tensor_copy(
-                    out=picked[:, :, :, :, j].rearrange("p q d v -> p d q v"),
-                    in_=planes[PACK * z + j].indirect(offsets[:]),
-                )
+                plane = planes[PACK * z + j]
+                by_piece = picked[:, :, :, :, j].rearrange("p q d v -> p d q v")
+                if PACK * z + j < len(planes) - 1:
+                    nc.vector.tensor_copy(out=by_piece, in_=plane.indirect(offsets[:]))
+                else:
+                    run = keep.tile([P, D // 2, QUARTERS, VQ], BF16, name="run", align_bytes=64)
+                    nc.vector.tensor_copy(out=run[:].rearrange("p d q v -> p (d q v)"), in_=plane.indirect(offsets[:, : S // 32]))
+                    nc.vector.tensor_copy(out=by_piece[:, D // 2 :], in_=plane.indirect(offsets[:, S // 32 :]))
+                    for q in range(QUARTERS):
+                        nc.scalar.copy(out=by_piece[:, : D // 2, q], in_=run[:, :, q])
             codes = keep.tile([P, S], U32, name="codes%d" % z, align_bytes=64)
             x_scales = keep.tile([P, S], U8, name="x_scales%d" % z, align_bytes=64)
             for q in range(QUARTERS):
@@ -113,7 +119,7 @@ def tile_picked_apool_none_e_kernel(tc, xT, w1_words, w1_scales, w2_words, w2_sc
                 )
 
         top = keep.tile([P, QUARTERS, VQ], F32, name="top")
-        shifted = keep.tile([P, QUARTERS, VQ, D], F32, name="shifted")
+        shifted = keep.tile([P, QUARTERS, VQ, D], F32, name="shifted", tag="shifted_then_inv")
         e = keep.tile([P, QUARTERS, VQ, D], F32, name="e")
         eh = keep.tile([P, D, QUARTERS, VQ], F32, name="eh")
         for step in range(QUARTERS + LAG):
@@ -130,7 +136,7 @@ def tile_picked_apool_none_e_kernel(tc, xT, w1_words, w1_scales, w2_words, w2_sc
                 nc.scalar.activation(out=e[:, q], in_=shifted[:, q], func=ACT.Exp)
 
         den = keep.tile([P, QUARTERS, VQ], F32, name="den")
-        inv = keep.tile([P, QUARTERS, VQ], F32, name="inv")
+        inv = keep.tile([P, QUARTERS, VQ], F32, name="inv", tag="shifted_then_inv")
         num_pairs = keep.tile([P, 2, QUARTERS, VQ], F32, name="num_pairs")
         num = keep.tile([P, V], F32, name="num")
         stretches = (slice(0, 1), slice(1, QUARTERS))

@@ -27,7 +27,7 @@ VQ = V // QUARTERS
 QC = D * VQ
 HALVES = 2
 HC = S // HALVES
-FIRST_LOAD_PLANES = 2
+PAIRED_PLANES = 4
 LAG = 2
 
 
@@ -59,8 +59,8 @@ def tile_picked_apool_none_e_kernel(tc, xT, w1_words, w1_scales, w2_words, w2_sc
         planes = []
         while len(planes) < PASSES * PACK:
             z, j0 = divmod(len(planes), PACK)
-            count = FIRST_LOAD_PLANES if not planes else 1
-            rows = keep.tile([P, count, T], F32, name="rows%d%d" % (z, j0), align_bytes=64)
+            count = 2 if len(planes) < PAIRED_PLANES else 1
+            rows = keep.tile([P, count, T], F32, name="rows%d%d" % (z, j0), tag="rows%d%d" % (z, j0), align_bytes=64)
             nc.sync.dma_start(out=rows[:], in_=x_rows[z, :, j0 : j0 + count, :])
             if not planes:
                 nc.sync.dma_start(offsets[:], offs)
@@ -75,18 +75,22 @@ def tile_picked_apool_none_e_kernel(tc, xT, w1_words, w1_scales, w2_words, w2_sc
         h_banks = [psum.tile([P, HC], F32, name="h_bank%d" % h) for h in range(HALVES)]
         for z in range(PASSES):
             picked = keep.tile([P, QUARTERS, D, VQ, PACK], BF16, name="picked%d" % z, align_bytes=64)
-            for j in range(PACK):
-                plane = planes[PACK * z + j]
-                by_piece = picked[:, :, :, :, j].rearrange("p q d v -> p d q v")
-                if PACK * z + j < len(planes) - 1:
-                    nc.vector.tensor_copy(out=by_piece, in_=plane.indirect(offsets[:]))
-                else:
-                    run = keep.tile([P, D // 2, QUARTERS, VQ], BF16, name="run", align_bytes=64)
+            by_piece = picked[:].rearrange("p q d v j -> p d q v j")
+            if z == 0:
+                for j0 in range(0, PACK, 2):
+                    runs = keep.tile([P, 2, D, QUARTERS, VQ], F32, name="runs%d" % j0, align_bytes=64)
+                    for i in range(2):
+                        nc.vector.tensor_copy(out=runs[:, i].rearrange("p d q v -> p (d q v)"), in_=planes[j0 + i].indirect(offsets[:]))
+                    nc.scalar.copy(out=by_piece[:, :, :, :, j0 : j0 + 2], in_=runs[:].rearrange("p j d q v -> p d q v j"))
+            else:
+                for j in range(PACK):
+                    plane = planes[PACK * z + j]
+                    run = keep.tile([P, D // 2, QUARTERS, VQ], BF16, name="run%d" % j, align_bytes=64)
                     nc.vector.tensor_copy(out=run[:].rearrange("p d q v -> p (d q v)"), in_=plane.indirect(offsets[:, : S // 32]))
-                    nc.vector.tensor_copy(out=by_piece[:, D // 2 :], in_=plane.indirect(offsets[:, S // 32 :]))
-                    for q in range(QUARTERS):
-                        nc.scalar.copy(out=by_piece[:, : D // 2, q], in_=run[:, :, q])
-            codes = keep.tile([P, S], U32, name="codes%d" % z, align_bytes=64)
+                    nc.vector.tensor_copy(out=by_piece[:, D // 2 :, :, :, j], in_=plane.indirect(offsets[:, S // 32 :]))
+                    for qs in [slice(0, QUARTERS)] if j < PACK - 1 else [slice(q, q + 1) for q in range(QUARTERS)]:
+                        nc.scalar.copy(out=by_piece[:, : D // 2, qs, :, j], in_=run[:, :, qs])
+            codes = keep.tile([P, S], U32, name="codes%d" % z, tag="rows10" if z == 0 else "codes", align_bytes=64)
             x_scales = keep.tile([P, S], U8, name="x_scales%d" % z, align_bytes=64)
             for q in range(QUARTERS):
                 cols = slice(q * QC, (q + 1) * QC)
@@ -152,8 +156,9 @@ def tile_picked_apool_none_e_kernel(tc, xT, w1_words, w1_scales, w2_words, w2_sc
             nc.gpsimd.tensor_tensor(out=num_pairs[:, :, qs, :], in0=eh[:, 0:2, qs, :], in1=eh[:, 2:4, qs, :], op=ALU.add)
             nc.vector.tensor_reduce(out=den[:, qs, :], in_=e[:, qs], axis=AX.X, op=ALU.add)
         nc.gpsimd.tensor_tensor(out=num[:], in0=num_pairs[:, 0].rearrange("p q v -> p (q v)"), in1=num_pairs[:, 1].rearrange("p q v -> p (q v)"), op=ALU.add)
-        for qs in stretches:
+        for qs in (slice(0, 1), slice(1, QUARTERS - 1), slice(QUARTERS - 1, QUARTERS)):
             nc.vector.reciprocal(out=inv[:, qs, :], in_=den[:, qs, :])
         result = keep.tile([P, V], F32, name="result")
-        nc.vector.tensor_tensor(out=result[:], in0=num[:], in1=inv[:].rearrange("p q v -> p (q v)"), op=ALU.mult)
+        for cols in (slice(0, V - VQ), slice(V - VQ, V)):
+            nc.vector.tensor_tensor(out=result[:, cols], in0=num[:, cols], in1=inv[:].rearrange("p q v -> p (q v)")[:, cols], op=ALU.mult)
         nc.sync.dma_start(out=out, in_=result[:])

@@ -1,6 +1,7 @@
 from contextlib import ExitStack
 
 import concourse.mybir as mybir
+from concourse.masks import make_identity
 
 K, T, S, V, N = 1024, 2048, 512, 128, 128
 FLOPS = 2 * 2 * K * N * S
@@ -22,13 +23,9 @@ PASSES = K // (P * PACK)
 D = S // V
 GROUPS = 4
 SCALE_ROWS = 4
-QUARTERS = 4
-VQ = V // QUARTERS
-QC = D * VQ
-HALVES = 2
-HC = S // HALVES
 PAIRED_PLANES = 4
-LAG = 2
+PARTS = 4
+MP = N // PARTS
 
 
 def tile_picked_apool_none_e_kernel(tc, xT, w1_words, w1_scales, w2_words, w2_scales, offs, out):
@@ -42,6 +39,7 @@ def tile_picked_apool_none_e_kernel(tc, xT, w1_words, w1_scales, w2_words, w2_sc
         w_words = [[keep.tile([P, N], I32, name="w_words%d%d" % (a, z), align_bytes=64) for z in range(PASSES)] for a in range(2)]
         w_scales = [keep.tile([P, PASSES, N], U8, name="w_scales%d" % a, align_bytes=64) for a in range(2)]
         staged = keep.tile([P, PASSES, N // 4], I32, name="staged")
+        identity = keep.tile([P, P], F32, name="identity")
 
         def live(g):
             return slice(32 * g, 32 * g + SCALE_ROWS)
@@ -53,6 +51,7 @@ def tile_picked_apool_none_e_kernel(tc, xT, w1_words, w1_scales, w2_words, w2_sc
             nc.scalar.dma_start(out=staged[live(g)], in_=scale_rows(w1_scales, g))
         for a in range(2):
             nc.gpsimd.memset(w_scales[a][:].rearrange("p z n -> p (z n)").bitcast(I32), 0)
+        make_identity(nc, identity[:])
         for g in range(GROUPS):
             nc.gpsimd.tensor_copy(out=w_scales[0][live(g)].bitcast(I32), in_=staged[live(g)])
 
@@ -71,94 +70,75 @@ def tile_picked_apool_none_e_kernel(tc, xT, w1_words, w1_scales, w2_words, w2_sc
             for a, words in enumerate((w1_words, w2_words)):
                 nc.sync.dma_start(out=w_words[a][z][:], in_=words[z].rearrange("p n r -> p (n r)").bitcast(I32))
 
-        s_banks = [psum.tile([P, D, VQ], F32, name="s_bank%d" % q) for q in range(QUARTERS)]
-        h_banks = [psum.tile([P, HC], F32, name="h_bank%d" % h) for h in range(HALVES)]
+        banks = [psum.tile([P, D, N], F32, name="bank%d" % a) for a in range(2)]
         for z in range(PASSES):
-            picked = keep.tile([P, QUARTERS, D, VQ, PACK], BF16, name="picked%d" % z, align_bytes=64)
-            by_piece = picked[:].rearrange("p q d v j -> p d q v j")
+            x_scales = keep.tile([P, S], U8, name="x_scales%d" % z, align_bytes=64)
             if z == 0:
+                picked = keep.tile([P, S, PACK], BF16, name="picked0", align_bytes=64)
                 for j0 in range(0, PACK, 2):
-                    runs = keep.tile([P, 2, D, QUARTERS, VQ], F32, name="runs%d" % j0, align_bytes=64)
+                    runs = keep.tile([P, 2, S], F32, name="runs%d" % j0, align_bytes=64)
                     for i in range(2):
-                        nc.vector.tensor_copy(out=runs[:, i].rearrange("p d q v -> p (d q v)"), in_=planes[j0 + i].indirect(offsets[:]))
-                    nc.scalar.copy(out=by_piece[:, :, :, :, j0 : j0 + 2], in_=runs[:].rearrange("p j d q v -> p d q v j"))
+                        nc.vector.tensor_copy(out=runs[:, i], in_=planes[j0 + i].indirect(offsets[:]))
+                    nc.scalar.copy(out=picked[:, :, j0 : j0 + 2], in_=runs[:].rearrange("p j s -> p s j"))
+                pieces = [picked[:, d * V : (d + 1) * V] for d in range(D)]
+                all_codes = keep.tile([P, S], U32, name="codes0", tag="rows10", align_bytes=64)
             else:
+                woven = [keep.tile([P, V, PACK], BF16, name="woven%d" % d, tag="woven%d" % d, align_bytes=64) for d in range(D // 2)]
+                stepped = keep.tile([P, S // 2, PACK], BF16, name="stepped", align_bytes=64)
                 for j in range(PACK):
                     plane = planes[PACK * z + j]
-                    run = keep.tile([P, D // 2, QUARTERS, VQ], BF16, name="run%d" % j, align_bytes=64)
-                    nc.vector.tensor_copy(out=run[:].rearrange("p d q v -> p (d q v)"), in_=plane.indirect(offsets[:, : S // 32]))
-                    nc.vector.tensor_copy(out=by_piece[:, D // 2 :, :, :, j], in_=plane.indirect(offsets[:, S // 32 :]))
-                    for qs in [slice(0, QUARTERS)] if j < PACK - 1 else [slice(q, q + 1) for q in range(QUARTERS)]:
-                        nc.scalar.copy(out=by_piece[:, : D // 2, qs, :, j], in_=run[:, :, qs])
-            codes = keep.tile([P, S], U32, name="codes%d" % z, tag="rows10" if z == 0 else "codes", align_bytes=64)
-            x_scales = keep.tile([P, S], U8, name="x_scales%d" % z, align_bytes=64)
-            for q in range(QUARTERS):
-                cols = slice(q * QC, (q + 1) * QC)
-                nc.vector.quantize_mx(
-                    out=codes[:, cols].bitcast(FP8X4),
-                    scales=x_scales[:, cols],
-                    in_=picked[:, q].rearrange("p d v j -> p (d v j)"),
-                )
-            for q in range(QUARTERS):
-                cols = slice(q * QC, (q + 1) * QC)
-                nc.tensor.matmul_mx(
-                    out=s_banks[q][:].rearrange("p d v -> p (d v)"),
-                    lhsT=w_words[0][z][:].bitcast(FP8X4),
-                    lhsT_scale=w_scales[0][:, z, :],
-                    rhs=codes[:, cols].bitcast(FP8X4),
-                    rhs_scale=x_scales[:, cols],
-                    start=(z == 0),
-                    stop=(z == PASSES - 1),
-                )
-            for h in range(HALVES):
-                cols = slice(h * HC, (h + 1) * HC)
-                nc.tensor.matmul_mx(
-                    out=h_banks[h][:],
-                    lhsT=w_words[1][z][:].bitcast(FP8X4),
-                    lhsT_scale=w_scales[1][:, z, :],
-                    rhs=codes[:, cols].bitcast(FP8X4),
-                    rhs_scale=x_scales[:, cols],
-                    start=(z == 0),
-                    stop=(z == PASSES - 1),
-                )
+                    run = keep.tile([P, S // 2], BF16, name="run%d" % j, align_bytes=64)
+                    for cols in [slice(0, S // 2)] if j < PACK - 1 else [slice(0, V), slice(V, 2 * V)]:
+                        nc.vector.tensor_copy(out=run[:, cols], in_=plane.indirect(offsets[:, cols.start // 16 : cols.stop // 16]))
+                    nc.vector.tensor_copy(out=stepped[:, :, j], in_=plane.indirect(offsets[:, S // 32 :]))
+                    for d in range(D // 2):
+                        nc.scalar.copy(out=woven[d][:, :, j], in_=run[:, d * V : (d + 1) * V])
+                pieces = [woven[0][:], woven[1][:], stepped[:, :V], stepped[:, V:]]
+            codes = []
+            for d in range(D):
+                if z == 0:
+                    codes.append(all_codes[:, d * V : (d + 1) * V])
+                else:
+                    codes.append(keep.tile([P, V], U32, name="codes1%d" % d, tag="woven%d" % (d - D // 2) if d >= D // 2 else "codes1%d" % d, align_bytes=64)[:])
+                nc.vector.quantize_mx(out=codes[d].bitcast(FP8X4), scales=x_scales[:, d * V : (d + 1) * V], in_=pieces[d].rearrange("p v j -> p (v j)"))
+            for a in range(2):
+                for d in range(D):
+                    cols = slice(d * V, (d + 1) * V)
+                    nc.tensor.matmul_mx(
+                        out=banks[a][:, d, :],
+                        lhsT=codes[d].bitcast(FP8X4),
+                        lhsT_scale=x_scales[:, cols],
+                        rhs=w_words[a][z][:].bitcast(FP8X4),
+                        rhs_scale=w_scales[a][:, z, :],
+                        start=(z == 0 and d == 0),
+                        stop=(z == PASSES - 1 and d == D - 1),
+                    )
 
-        top = keep.tile([P, QUARTERS, VQ], F32, name="top")
-        shifted = keep.tile([P, QUARTERS, VQ, D], F32, name="shifted", tag="shifted_then_inv")
-        e = keep.tile([P, QUARTERS, VQ, D], F32, name="e")
-        eh = keep.tile([P, D, QUARTERS, VQ], F32, name="eh")
-        for step in range(QUARTERS + LAG):
-            if step < QUARTERS:
-                nc.vector.tensor_reduce(out=top[:, step, :], in_=s_banks[step][:].rearrange("p d v -> p v d"), axis=AX.X, op=ALU.max)
-            if step >= LAG:
-                q = step - LAG
-                nc.vector.tensor_tensor(
-                    out=shifted[:, q],
-                    in0=s_banks[q][:].rearrange("p d v -> p v d"),
-                    in1=top[:, q, :].unsqueeze(2).to_broadcast([P, VQ, D]),
-                    op=ALU.subtract,
-                )
-                nc.scalar.activation(out=e[:, q], in_=shifted[:, q], func=ACT.Exp)
-
-        den = keep.tile([P, QUARTERS, VQ], F32, name="den")
-        inv = keep.tile([P, QUARTERS, VQ], F32, name="inv", tag="shifted_then_inv")
-        num_pairs = keep.tile([P, 2, QUARTERS, VQ], F32, name="num_pairs")
-        num = keep.tile([P, V], F32, name="num")
-        stretches = (slice(0, 1), slice(1, QUARTERS))
-        for qs in stretches:
-            for q in range(qs.start, qs.stop):
-                h, q_in_half = divmod(q, QUARTERS // HALVES)
-                nc.vector.tensor_tensor(
-                    out=eh[:, :, q, :].rearrange("p d v -> p v d"),
-                    in0=h_banks[h][:].rearrange("p (q d v) -> p q v d", d=D, v=VQ)[:, q_in_half],
-                    in1=e[:, q],
-                    op=ALU.mult,
-                )
-            nc.gpsimd.tensor_tensor(out=num_pairs[:, :, qs, :], in0=eh[:, 0:2, qs, :], in1=eh[:, 2:4, qs, :], op=ALU.add)
-            nc.vector.tensor_reduce(out=den[:, qs, :], in_=e[:, qs], axis=AX.X, op=ALU.add)
-        nc.gpsimd.tensor_tensor(out=num[:], in0=num_pairs[:, 0].rearrange("p q v -> p (q v)"), in1=num_pairs[:, 1].rearrange("p q v -> p (q v)"), op=ALU.add)
-        for qs in (slice(0, 1), slice(1, QUARTERS - 1), slice(QUARTERS - 1, QUARTERS)):
-            nc.vector.reciprocal(out=inv[:, qs, :], in_=den[:, qs, :])
+        top = keep.tile([P, N], F32, name="top")
+        shifted = keep.tile([P, D, N], F32, name="shifted")
+        e = keep.tile([P, D, N], F32, name="e")
+        eh = keep.tile([P, D, N], F32, name="eh")
+        parts = [slice(i * MP, (i + 1) * MP) for i in range(PARTS)]
+        for step in range(PARTS + 2):
+            if step < PARTS:
+                m = parts[step]
+                nc.vector.tensor_reduce(out=top[:, m], in_=banks[0][:, :, m].rearrange("p d m -> p m d"), axis=AX.X, op=ALU.max)
+            if step >= 2:
+                m = parts[step - 2]
+                nc.vector.tensor_tensor(out=shifted[:, :, m], in0=banks[0][:, :, m], in1=top[:, m].unsqueeze(1).to_broadcast([P, D, MP]), op=ALU.subtract)
+                nc.scalar.activation(out=e[:, :, m], in_=shifted[:, :, m], func=ACT.Exp)
+        for m in (slice(0, N // 2), slice(N // 2, N)):
+            nc.vector.tensor_tensor(out=eh[:, :, m], in0=banks[1][:, :, m], in1=e[:, :, m], op=ALU.mult)
+        den = psum.tile([P, V], F32, name="den")
+        num = psum.tile([P, V], F32, name="num")
+        for total, terms in ((den, e), (num, eh)):
+            for d in range(D):
+                nc.tensor.matmul(total[:], terms[:, d, :], identity[:], start=(d == 0), stop=(d == D - 1), is_transpose=True)
+        inv = keep.tile([P, V], F32, name="inv")
         result = keep.tile([P, V], F32, name="result")
-        for cols in (slice(0, V - VQ), slice(V - VQ, V)):
-            nc.vector.tensor_tensor(out=result[:, cols], in0=num[:, cols], in1=inv[:].rearrange("p q v -> p (q v)")[:, cols], op=ALU.mult)
+        halves = (slice(0, V // 2), slice(V // 2, V))
+        for v in halves:
+            nc.vector.reciprocal(out=inv[:, v], in_=den[:, v])
+        for v in halves:
+            nc.vector.tensor_tensor(out=result[:, v], in0=num[:, v], in1=inv[:, v], op=ALU.mult)
         nc.sync.dma_start(out=out, in_=result[:])

@@ -24,8 +24,7 @@ D = S // V
 GROUPS = 4
 SCALE_ROWS = 4
 PAIRED_PLANES = 4
-PARTS = 4
-MP = N // PARTS
+CAP = 40.0
 
 
 def tile_picked_apool_none_e_kernel(tc, xT, w1_words, w1_scales, w2_words, w2_scales, offs, out):
@@ -70,7 +69,9 @@ def tile_picked_apool_none_e_kernel(tc, xT, w1_words, w1_scales, w2_words, w2_sc
             for a, words in enumerate((w1_words, w2_words)):
                 nc.sync.dma_start(out=w_words[a][z][:], in_=words[z].rearrange("p n r -> p (n r)").bitcast(I32))
 
-        banks = [psum.tile([P, D, N], F32, name="bank%d" % a) for a in range(2)]
+        s_first = psum.tile([P, D - 1, N], F32, name="s_first")
+        s_last = psum.tile([P, N], F32, name="s_last")
+        h_bank = psum.tile([P, D, N], F32, name="h_bank")
         for z in range(PASSES):
             x_scales = keep.tile([P, S], U8, name="x_scales%d" % z, align_bytes=64)
             if z == 0:
@@ -104,31 +105,44 @@ def tile_picked_apool_none_e_kernel(tc, xT, w1_words, w1_scales, w2_words, w2_sc
             for a in range(2):
                 for d in range(D):
                     cols = slice(d * V, (d + 1) * V)
+                    if a == 1:
+                        target, first, last = h_bank[:, d, :], 0, D - 1
+                    elif d < D - 1:
+                        target, first, last = s_first[:, d, :], 0, D - 2
+                    else:
+                        target, first, last = s_last[:], d, d
                     nc.tensor.matmul_mx(
-                        out=banks[a][:, d, :],
+                        out=target,
                         lhsT=codes[d].bitcast(FP8X4),
                         lhsT_scale=x_scales[:, cols],
                         rhs=w_words[a][z][:].bitcast(FP8X4),
                         rhs_scale=w_scales[a][:, z, :],
-                        start=(z == 0 and d == 0),
-                        stop=(z == PASSES - 1 and d == D - 1),
+                        start=(z == 0 and d == first),
+                        stop=(z == PASSES - 1 and d == last),
                     )
 
         top = keep.tile([P, N], F32, name="top")
         shifted = keep.tile([P, D, N], F32, name="shifted")
         e = keep.tile([P, D, N], F32, name="e")
         eh = keep.tile([P, D, N], F32, name="eh")
-        parts = [slice(i * MP, (i + 1) * MP) for i in range(PARTS)]
-        for step in range(PARTS + 2):
-            if step < PARTS:
-                m = parts[step]
-                nc.vector.tensor_reduce(out=top[:, m], in_=banks[0][:, :, m].rearrange("p d m -> p m d"), axis=AX.X, op=ALU.max)
-            if step >= 2:
-                m = parts[step - 2]
-                nc.vector.tensor_tensor(out=shifted[:, :, m], in0=banks[0][:, :, m], in1=top[:, m].unsqueeze(1).to_broadcast([P, D, MP]), op=ALU.subtract)
-                nc.scalar.activation(out=e[:, :, m], in_=shifted[:, :, m], func=ACT.Exp)
-        for m in (slice(0, N // 2), slice(N // 2, N)):
-            nc.vector.tensor_tensor(out=eh[:, :, m], in0=banks[1][:, :, m], in1=e[:, :, m], op=ALU.mult)
+        parts = (slice(0, N // 2), slice(N // 2, N))
+        capped = keep.tile([P, N], F32, name="capped")
+        for m in parts:
+            nc.vector.tensor_reduce(out=top[:, m], in_=s_first[:, :, m].rearrange("p d m -> p m d"), axis=AX.X, op=ALU.max)
+
+        def shift_and_exp(ds, m):
+            spread = top[:, m].unsqueeze(1).to_broadcast([P, ds.stop - ds.start, m.stop - m.start])
+            nc.vector.tensor_tensor(out=shifted[:, ds, m], in0=s_first[:, ds, m], in1=spread, op=ALU.subtract)
+            nc.scalar.activation(out=e[:, ds, m], in_=shifted[:, ds, m], func=ACT.Exp)
+
+        shift_and_exp(slice(0, D - 1), parts[0])
+        nc.vector.tensor_tensor(out=shifted[:, D - 1], in0=s_last[:], in1=top[:], op=ALU.subtract)
+        for d in range(D - 1):
+            shift_and_exp(slice(d, d + 1), parts[1])
+        nc.vector.tensor_scalar_min(out=capped[:], in0=shifted[:, D - 1], scalar1=CAP)
+        nc.scalar.activation(out=e[:, D - 1], in_=capped[:], func=ACT.Exp)
+        for ds in (slice(0, D // 2), slice(D // 2, D)):
+            nc.vector.tensor_tensor(out=eh[:, ds], in0=h_bank[:, ds], in1=e[:, ds], op=ALU.mult)
         den = psum.tile([P, V], F32, name="den")
         num = psum.tile([P, V], F32, name="num")
         for total, terms in ((den, e), (num, eh)):
@@ -136,7 +150,7 @@ def tile_picked_apool_none_e_kernel(tc, xT, w1_words, w1_scales, w2_words, w2_sc
                 nc.tensor.matmul(total[:], terms[:, d, :], identity[:], start=(d == 0), stop=(d == D - 1), is_transpose=True)
         inv = keep.tile([P, V], F32, name="inv")
         result = keep.tile([P, V], F32, name="result")
-        halves = (slice(0, V // 2), slice(V // 2, V))
+        halves = (slice(0, 3 * V // 4), slice(3 * V // 4, V))
         for v in halves:
             nc.vector.reciprocal(out=inv[:, v], in_=den[:, v])
         for v in halves:

@@ -72,35 +72,24 @@ def tile_picked_apool_none_e_kernel(tc, xT, w1_words, w1_scales, w2_words, w2_sc
         s_first = psum.tile([P, D - 1, N], F32, name="s_first")
         s_last = psum.tile([P, N], F32, name="s_last")
         h_bank = psum.tile([P, D, N], F32, name="h_bank")
+        half = S // 2
         for z in range(PASSES):
             x_scales = keep.tile([P, S], U8, name="x_scales%d" % z, align_bytes=64)
-            if z == 0:
-                picked = keep.tile([P, S, PACK], BF16, name="picked0", align_bytes=64)
-                for j0 in range(0, PACK, 2):
-                    runs = keep.tile([P, 2, S], F32, name="runs%d" % j0, align_bytes=64)
-                    for i in range(2):
-                        nc.vector.tensor_copy(out=runs[:, i], in_=planes[j0 + i].indirect(offsets[:]))
-                    nc.scalar.copy(out=picked[:, :, j0 : j0 + 2], in_=runs[:].rearrange("p j s -> p s j"))
-                pieces = [picked[:, d * V : (d + 1) * V] for d in range(D)]
-                all_codes = keep.tile([P, S], U32, name="codes0", tag="rows10", align_bytes=64)
-            else:
-                woven = [keep.tile([P, V, PACK], BF16, name="woven%d" % d, tag="woven%d" % d, align_bytes=64) for d in range(D // 2)]
-                stepped = keep.tile([P, S // 2, PACK], BF16, name="stepped", align_bytes=64)
-                for j in range(PACK):
-                    plane = planes[PACK * z + j]
-                    run = keep.tile([P, S // 2], BF16, name="run%d" % j, align_bytes=64)
-                    for cols in [slice(0, S // 2)] if j < PACK - 1 else [slice(0, V), slice(V, 2 * V)]:
-                        nc.vector.tensor_copy(out=run[:, cols], in_=plane.indirect(offsets[:, cols.start // 16 : cols.stop // 16]))
-                    nc.vector.tensor_copy(out=stepped[:, :, j], in_=plane.indirect(offsets[:, S // 32 :]))
-                    for d in range(D // 2):
-                        nc.scalar.copy(out=woven[d][:, :, j], in_=run[:, d * V : (d + 1) * V])
-                pieces = [woven[0][:], woven[1][:], stepped[:, :V], stepped[:, V:]]
+            stepped = keep.tile([P, half, PACK], BF16, name="stepped%d" % z, align_bytes=64)
+            woven = [keep.tile([P, V, PACK], BF16, name="woven%d%d" % (z, i), align_bytes=64) for i in range(D // 2)]
+            for j in range(PACK):
+                plane = planes[PACK * z + j]
+                nc.vector.tensor_copy(out=stepped[:, :, j], in_=plane.indirect(offsets[:, : half // 16]))
+                run = keep.tile([P, half], F32 if PACK * z + j < PAIRED_PLANES else BF16, name="run%d%d" % (z, j), align_bytes=64)
+                last_plane = z == PASSES - 1 and j == PACK - 1
+                for cols in [slice(0, V), slice(V, 2 * V)] if last_plane else [slice(0, half)]:
+                    nc.scalar.activation(out=run[:, cols], in_=plane.indirect(offsets[:, (half + cols.start) // 16 : (half + cols.stop) // 16]), func=ACT.Copy)
+                for i in range(D // 2):
+                    nc.scalar.copy(out=woven[i][:, :, j], in_=run[:, i * V : (i + 1) * V])
+            pieces = [stepped[:, :V], stepped[:, V:], woven[0][:], woven[1][:]]
             codes = []
             for d in range(D):
-                if z == 0:
-                    codes.append(all_codes[:, d * V : (d + 1) * V])
-                else:
-                    codes.append(keep.tile([P, V], U32, name="codes1%d" % d, tag="woven%d" % (d - D // 2) if d >= D // 2 else "codes1%d" % d, align_bytes=64)[:])
+                codes.append(keep.tile([P, V], U32, name="codes%d%d" % (z, d), align_bytes=64)[:])
                 nc.vector.quantize_mx(out=codes[d].bitcast(FP8X4), scales=x_scales[:, d * V : (d + 1) * V], in_=pieces[d].rearrange("p v j -> p (v j)"))
             for a in range(2):
                 for d in range(D):

@@ -23,7 +23,7 @@ PASSES = K // (P * PACK)
 D = S // V
 GROUPS = 4
 SCALE_ROWS = 4
-PAIRED_PLANES = 4
+LOADS = (4, 2, 1, 1)
 CAP = 40.0
 
 
@@ -51,13 +51,14 @@ def tile_picked_apool_none_e_kernel(tc, xT, w1_words, w1_scales, w2_words, w2_sc
         for a in range(2):
             nc.gpsimd.memset(w_scales[a][:].rearrange("p z n -> p (z n)").bitcast(I32), 0)
         make_identity(nc, identity[:])
+        warm = keep.tile([P, 1], F32, name="warm")
+        nc.scalar.activation(out=warm[:], in_=identity[:, 0:1], func=ACT.Exp)
         for g in range(GROUPS):
             nc.gpsimd.tensor_copy(out=w_scales[0][live(g)].bitcast(I32), in_=staged[live(g)])
 
         planes = []
-        while len(planes) < PASSES * PACK:
+        for count in LOADS:
             z, j0 = divmod(len(planes), PACK)
-            count = 2 if len(planes) < PAIRED_PLANES else 1
             rows = keep.tile([P, count, T], F32, name="rows%d%d" % (z, j0), tag="rows%d%d" % (z, j0), align_bytes=64)
             nc.sync.dma_start(out=rows[:], in_=x_rows[z, :, j0 : j0 + count, :])
             if not planes:
@@ -75,18 +76,35 @@ def tile_picked_apool_none_e_kernel(tc, xT, w1_words, w1_scales, w2_words, w2_sc
         half = S // 2
         for z in range(PASSES):
             x_scales = keep.tile([P, S], U8, name="x_scales%d" % z, align_bytes=64)
-            stepped = keep.tile([P, half, PACK], BF16, name="stepped%d" % z, align_bytes=64)
-            woven = [keep.tile([P, V, PACK], BF16, name="woven%d%d" % (z, i), align_bytes=64) for i in range(D // 2)]
-            for j in range(PACK):
-                plane = planes[PACK * z + j]
-                nc.vector.tensor_copy(out=stepped[:, :, j], in_=plane.indirect(offsets[:, : half // 16]))
-                run = keep.tile([P, half], F32 if PACK * z + j < PAIRED_PLANES else BF16, name="run%d%d" % (z, j), align_bytes=64)
-                last_plane = z == PASSES - 1 and j == PACK - 1
-                for cols in [slice(0, V), slice(V, 2 * V)] if last_plane else [slice(0, half)]:
-                    nc.scalar.activation(out=run[:, cols], in_=plane.indirect(offsets[:, (half + cols.start) // 16 : (half + cols.stop) // 16]), func=ACT.Copy)
-                for i in range(D // 2):
-                    nc.scalar.copy(out=woven[i][:, :, j], in_=run[:, i * V : (i + 1) * V])
-            pieces = [stepped[:, :V], stepped[:, V:], woven[0][:], woven[1][:]]
+            if z == 0:
+                runs = keep.tile([P, PACK, S], F32, name="runs", align_bytes=64)
+                picked = keep.tile([P, S, PACK], BF16, name="picked", align_bytes=64)
+                for j in range(PACK):
+                    if j % 2 == 0:
+                        nc.vector.tensor_copy(out=runs[:, j], in_=planes[j].indirect(offsets[:]))
+                    else:
+                        nc.scalar.activation(out=runs[:, j], in_=planes[j].indirect(offsets[:]), func=ACT.Copy)
+                nc.vector.tensor_copy(out=picked[:], in_=runs[:].rearrange("p j s -> p s j"))
+                pieces = [picked[:, d * V : (d + 1) * V] for d in range(D)]
+            else:
+                stepped = keep.tile([P, half, PACK], BF16, name="stepped", align_bytes=64)
+                woven = keep.tile([P, half, PACK], BF16, name="woven", align_bytes=64)
+                pair = keep.tile([P, 2, half], F32, name="pair", align_bytes=64)
+                for j in range(PACK):
+                    plane = planes[PACK * z + j]
+                    nc.vector.tensor_copy(out=stepped[:, :, j], in_=plane.indirect(offsets[:, : half // 16]))
+                    if j < 2:
+                        nc.scalar.activation(out=pair[:, j], in_=plane.indirect(offsets[:, half // 16 :]), func=ACT.Copy)
+                        if j == 1:
+                            nc.vector.tensor_copy(out=woven[:, :, 0:2], in_=pair[:].rearrange("p j s -> p s j"))
+                        continue
+                    run = keep.tile([P, half], BF16, name="run%d" % j, align_bytes=64)
+                    parts_of_run = [slice(0, V), slice(V, 2 * V)] if j == PACK - 1 else [slice(0, half)]
+                    for cols in parts_of_run:
+                        nc.scalar.activation(out=run[:, cols], in_=plane.indirect(offsets[:, (half + cols.start) // 16 : (half + cols.stop) // 16]), func=ACT.Copy)
+                    for cols in parts_of_run:
+                        nc.scalar.copy(out=woven[:, cols, j], in_=run[:, cols])
+                pieces = [stepped[:, :V], stepped[:, V:], woven[:, :V], woven[:, V:]]
             codes = []
             for d in range(D):
                 codes.append(keep.tile([P, V], U32, name="codes%d%d" % (z, d), align_bytes=64)[:])

@@ -24,6 +24,7 @@ D = S // V
 GROUPS = 4
 SCALE_ROWS = 4
 LOADS = (4, 2, 1, 1)
+FIRST_FEATURES = 48
 CAP = 40.0
 
 
@@ -88,23 +89,23 @@ def tile_picked_apool_none_e_kernel(tc, xT, w1_words, w1_scales, w2_words, w2_sc
                 pieces = [picked[:, d * V : (d + 1) * V] for d in range(D)]
             else:
                 stepped = keep.tile([P, half, PACK], BF16, name="stepped", align_bytes=64)
-                woven = keep.tile([P, half, PACK], BF16, name="woven", align_bytes=64)
+                woven = [keep.tile([P, V, PACK], BF16, name="woven%d" % i, align_bytes=64) for i in range(D // 2)]
                 pair = keep.tile([P, 2, half], F32, name="pair", align_bytes=64)
                 for j in range(PACK):
                     plane = planes[PACK * z + j]
                     nc.vector.tensor_copy(out=stepped[:, :, j], in_=plane.indirect(offsets[:, : half // 16]))
                     if j < 2:
                         nc.scalar.activation(out=pair[:, j], in_=plane.indirect(offsets[:, half // 16 :]), func=ACT.Copy)
-                        if j == 1:
-                            nc.vector.tensor_copy(out=woven[:, :, 0:2], in_=pair[:].rearrange("p j s -> p s j"))
+                        for i in range(D // 2) if j == 1 else []:
+                            nc.vector.tensor_copy(out=woven[i][:, :, 0:2], in_=pair[:, :, i * V : (i + 1) * V].rearrange("p j s -> p s j"))
                         continue
                     run = keep.tile([P, half], BF16, name="run%d" % j, align_bytes=64)
                     parts_of_run = [slice(0, V), slice(V, 2 * V)] if j == PACK - 1 else [slice(0, half)]
                     for cols in parts_of_run:
                         nc.scalar.activation(out=run[:, cols], in_=plane.indirect(offsets[:, (half + cols.start) // 16 : (half + cols.stop) // 16]), func=ACT.Copy)
-                    for cols in parts_of_run:
-                        nc.scalar.copy(out=woven[:, cols, j], in_=run[:, cols])
-                pieces = [stepped[:, :V], stepped[:, V:], woven[:, :V], woven[:, V:]]
+                    for i in range(D // 2):
+                        nc.scalar.copy(out=woven[i][:, :, j], in_=run[:, i * V : (i + 1) * V])
+                pieces = [stepped[:, :V], stepped[:, V:], woven[0][:], woven[1][:]]
             codes = []
             for d in range(D):
                 codes.append(keep.tile([P, V], U32, name="codes%d%d" % (z, d), align_bytes=64)[:])
@@ -132,7 +133,7 @@ def tile_picked_apool_none_e_kernel(tc, xT, w1_words, w1_scales, w2_words, w2_sc
         shifted = keep.tile([P, D, N], F32, name="shifted")
         e = keep.tile([P, D, N], F32, name="e")
         eh = keep.tile([P, D, N], F32, name="eh")
-        parts = (slice(0, N // 2), slice(N // 2, N))
+        parts = (slice(0, FIRST_FEATURES), slice(FIRST_FEATURES, N))
         capped = keep.tile([P, N], F32, name="capped")
         for m in parts:
             nc.vector.tensor_reduce(out=top[:, m], in_=s_first[:, :, m].rearrange("p d m -> p m d"), axis=AX.X, op=ALU.max)
@@ -143,7 +144,8 @@ def tile_picked_apool_none_e_kernel(tc, xT, w1_words, w1_scales, w2_words, w2_sc
             nc.scalar.activation(out=e[:, ds, m], in_=shifted[:, ds, m], func=ACT.Exp)
 
         shift_and_exp(slice(0, D - 1), parts[0])
-        nc.vector.tensor_tensor(out=shifted[:, D - 1], in0=s_last[:], in1=top[:], op=ALU.subtract)
+        for m in parts:
+            nc.vector.tensor_tensor(out=shifted[:, D - 1, m], in0=s_last[:, m], in1=top[:, m], op=ALU.subtract)
         for d in range(D - 1):
             shift_and_exp(slice(d, d + 1), parts[1])
         nc.vector.tensor_scalar_min(out=capped[:], in0=shifted[:, D - 1], scalar1=CAP)

@@ -36,9 +36,8 @@ def tile_picked_apool_none_e_kernel(tc, xT, w1_words, w1_scales, w2_words, w2_sc
 
         offsets = keep.tile([P, S // 16], U16, name="offsets")
         x_rows = xT.rearrange("(z p j) t -> z p j t", z=PASSES, j=PACK)
-        w_words = [[keep.tile([P, N], I32, name="w_words%d%d" % (a, z), align_bytes=64) for z in range(PASSES)] for a in range(2)]
+        w_words = [keep.tile([P, PASSES, N], I32, name="w_words%d" % a, align_bytes=64) for a in range(2)]
         w_scales = [keep.tile([P, PASSES, N], U8, name="w_scales%d" % a, align_bytes=64) for a in range(2)]
-        staged = keep.tile([P, PASSES, N // 4], I32, name="staged")
         identity = keep.tile([P, P], F32, name="identity")
 
         def live(g):
@@ -47,15 +46,11 @@ def tile_picked_apool_none_e_kernel(tc, xT, w1_words, w1_scales, w2_words, w2_sc
         def scale_rows(scales, g):
             return scales[:, SCALE_ROWS * g : SCALE_ROWS * (g + 1), :].rearrange("z r n -> r z n").bitcast(I32)
 
-        for g in range(GROUPS):
-            nc.scalar.dma_start(out=staged[live(g)], in_=scale_rows(w1_scales, g))
         for a in range(2):
             nc.gpsimd.memset(w_scales[a][:].rearrange("p z n -> p (z n)").bitcast(I32), 0)
         make_identity(nc, identity[:])
         warm = keep.tile([P, 1], F32, name="warm")
         nc.scalar.activation(out=warm[:], in_=identity[:, 0:1], func=ACT.Exp)
-        for g in range(GROUPS):
-            nc.gpsimd.tensor_copy(out=w_scales[0][live(g)].bitcast(I32), in_=staged[live(g)])
 
         planes = []
         for count in LOADS:
@@ -65,11 +60,10 @@ def tile_picked_apool_none_e_kernel(tc, xT, w1_words, w1_scales, w2_words, w2_sc
             if not planes:
                 nc.sync.dma_start(offsets[:], offs)
             planes.extend(rows[:, i, :] for i in range(count))
-        for g in range(GROUPS):
-            nc.sync.dma_start(out=w_scales[1][live(g)].bitcast(I32), in_=scale_rows(w2_scales, g))
-        for z in range(PASSES):
-            for a, words in enumerate((w1_words, w2_words)):
-                nc.sync.dma_start(out=w_words[a][z][:], in_=words[z].rearrange("p n r -> p (n r)").bitcast(I32))
+        for a, (words, scales) in enumerate(((w1_words, w1_scales), (w2_words, w2_scales))):
+            nc.sync.dma_start(out=w_words[a][:], in_=words.rearrange("z p n r -> p z (n r)").bitcast(I32))
+            for g in range(GROUPS):
+                nc.sync.dma_start(out=w_scales[a][live(g)].bitcast(I32), in_=scale_rows(scales, g))
 
         s_first = psum.tile([P, D - 1, N], F32, name="s_first")
         s_last = psum.tile([P, N], F32, name="s_last")
@@ -108,7 +102,7 @@ def tile_picked_apool_none_e_kernel(tc, xT, w1_words, w1_scales, w2_words, w2_sc
                 pieces = [stepped[:, :V], stepped[:, V:], woven[0][:], woven[1][:]]
             codes = []
             for d in range(D):
-                codes.append(keep.tile([P, V], U32, name="codes%d%d" % (z, d), align_bytes=64)[:])
+                codes.append(keep.tile([P, V], U32, name="codes%d%d" % (z, d), tag="codes%d%d" % (z, d), align_bytes=64)[:])
                 nc.vector.quantize_mx(out=codes[d].bitcast(FP8X4), scales=x_scales[:, d * V : (d + 1) * V], in_=pieces[d].rearrange("p v j -> p (v j)"))
             for a in range(2):
                 for d in range(D):
@@ -123,7 +117,7 @@ def tile_picked_apool_none_e_kernel(tc, xT, w1_words, w1_scales, w2_words, w2_sc
                         out=target,
                         lhsT=codes[d].bitcast(FP8X4),
                         lhsT_scale=x_scales[:, cols],
-                        rhs=w_words[a][z][:].bitcast(FP8X4),
+                        rhs=w_words[a][:, z, :].bitcast(FP8X4),
                         rhs_scale=w_scales[a][:, z, :],
                         start=(z == 0 and d == first),
                         stop=(z == PASSES - 1 and d == last),
@@ -131,7 +125,7 @@ def tile_picked_apool_none_e_kernel(tc, xT, w1_words, w1_scales, w2_words, w2_sc
 
         top = keep.tile([P, N], F32, name="top")
         shifted = keep.tile([P, D, N], F32, name="shifted")
-        e = keep.tile([P, D, N], F32, name="e")
+        e = keep.tile([P, D, N], F32, name="e", tag="codes00", align_bytes=64)
         eh = keep.tile([P, D, N], F32, name="eh")
         parts = (slice(0, FIRST_FEATURES), slice(FIRST_FEATURES, N))
         capped = keep.tile([P, N], F32, name="capped")
@@ -150,8 +144,8 @@ def tile_picked_apool_none_e_kernel(tc, xT, w1_words, w1_scales, w2_words, w2_sc
             shift_and_exp(slice(d, d + 1), parts[1])
         nc.vector.tensor_scalar_min(out=capped[:], in0=shifted[:, D - 1], scalar1=CAP)
         nc.scalar.activation(out=e[:, D - 1], in_=capped[:], func=ACT.Exp)
-        for ds in (slice(0, D // 2), slice(D // 2, D)):
-            nc.vector.tensor_tensor(out=eh[:, ds], in0=h_bank[:, ds], in1=e[:, ds], op=ALU.mult)
+        for ds, m in ((slice(0, D - 1), parts[0]), (slice(0, D - 2), parts[1]), (slice(D - 2, D - 1), parts[1]), (slice(D - 1, D), slice(0, N))):
+            nc.vector.tensor_tensor(out=eh[:, ds, m], in0=h_bank[:, ds, m], in1=e[:, ds, m], op=ALU.mult)
         den = psum.tile([P, V], F32, name="den")
         num = psum.tile([P, V], F32, name="num")
         for total, terms in ((den, e), (num, eh)):

@@ -67,7 +67,15 @@ def tile_picked_apool_none_e_kernel(tc, xT, w1_words, w1_scales, w2_words, w2_sc
 
         s_first = psum.tile([P, D - 1, N], F32, name="s_first")
         s_last = psum.tile([P, N], F32, name="s_last")
-        h_bank = psum.tile([P, D, N], F32, name="h_bank")
+        h_banks = [psum.tile([P, D // 2, N], F32, name="h_bank%d" % i) for i in range(2)]
+        quantised = []
+        laid_out = []
+
+        def quantise(z, d, tag):
+            codes, x_scales = quantised[z]
+            codes.setdefault(d, keep.tile([P, V], U32, name="codes%d%d" % (z, d), tag=tag, align_bytes=64)[:])
+            nc.vector.quantize_mx(out=codes[d].bitcast(FP8X4), scales=x_scales[:, d * V : (d + 1) * V], in_=laid_out[z][d].rearrange("p v j -> p (v j)"))
+
         half = S // 2
         for z in range(PASSES):
             x_scales = keep.tile([P, S], U8, name="x_scales%d" % z, align_bytes=64)
@@ -93,35 +101,40 @@ def tile_picked_apool_none_e_kernel(tc, xT, w1_words, w1_scales, w2_words, w2_sc
                         for i in range(D // 2) if j == 1 else []:
                             nc.vector.tensor_copy(out=woven[i][:, :, 0:2], in_=pair[:, :, i * V : (i + 1) * V].rearrange("p j s -> p s j"))
                         continue
-                    run = keep.tile([P, half], BF16, name="run%d" % j, align_bytes=64)
+                    run = keep.tile([P, half], BF16, name="run%d" % j, tag="run%d" % j, align_bytes=64)
                     parts_of_run = [slice(0, V), slice(V, 2 * V)] if j == PACK - 1 else [slice(0, half)]
                     for cols in parts_of_run:
                         nc.scalar.activation(out=run[:, cols], in_=plane.indirect(offsets[:, (half + cols.start) // 16 : (half + cols.stop) // 16]), func=ACT.Copy)
                     for i in range(D // 2):
                         nc.scalar.copy(out=woven[i][:, :, j], in_=run[:, i * V : (i + 1) * V])
                 pieces = [stepped[:, :V], stepped[:, V:], woven[0][:], woven[1][:]]
-            codes = []
-            for d in range(D):
-                codes.append(keep.tile([P, V], U32, name="codes%d%d" % (z, d), tag="codes%d%d" % (z, d), align_bytes=64)[:])
-                nc.vector.quantize_mx(out=codes[d].bitcast(FP8X4), scales=x_scales[:, d * V : (d + 1) * V], in_=pieces[d].rearrange("p v j -> p (v j)"))
-            for a in range(2):
-                for d in range(D):
-                    cols = slice(d * V, (d + 1) * V)
-                    if a == 1:
-                        target, first, last = h_bank[:, d, :], 0, D - 1
-                    elif d < D - 1:
-                        target, first, last = s_first[:, d, :], 0, D - 2
-                    else:
-                        target, first, last = s_last[:], d, d
-                    nc.tensor.matmul_mx(
-                        out=target,
-                        lhsT=codes[d].bitcast(FP8X4),
-                        lhsT_scale=x_scales[:, cols],
-                        rhs=w_words[a][:, z, :].bitcast(FP8X4),
-                        rhs_scale=w_scales[a][:, z, :],
-                        start=(z == 0 and d == first),
-                        stop=(z == PASSES - 1 and d == last),
-                    )
+            laid_out.append(pieces)
+            quantised.append(({}, x_scales))
+            for d in range(D - 1):
+                quantise(z, d, "codes%d%d" % (z, d))
+        quantise(0, D - 1, "run%d" % (PACK - 1))
+        quantise(1, D - 1, "codes13")
+
+        def one_pass(a, z, d, target, start, stop):
+            codes, x_scales = quantised[z]
+            nc.tensor.matmul_mx(
+                out=target,
+                lhsT=codes[d].bitcast(FP8X4),
+                lhsT_scale=x_scales[:, d * V : (d + 1) * V],
+                rhs=w_words[a][:, z, :].bitcast(FP8X4),
+                rhs_scale=w_scales[a][:, z, :],
+                start=start,
+                stop=stop,
+            )
+
+        for z in range(PASSES):
+            for d in range(D - 1):
+                one_pass(0, z, d, s_first[:, d, :], z == 0 and d == 0, z == PASSES - 1 and d == D - 2)
+        for z in range(PASSES):
+            one_pass(0, z, D - 1, s_last[:], z == 0, z == PASSES - 1)
+        for d in range(D):
+            for z in range(PASSES):
+                one_pass(1, z, d, h_banks[d // 2][:, d % 2, :], z == 0 and d % 2 == 0, z == PASSES - 1 and d % 2 == 1)
 
         top = keep.tile([P, N], F32, name="top")
         shifted = keep.tile([P, D, N], F32, name="shifted")
@@ -144,8 +157,8 @@ def tile_picked_apool_none_e_kernel(tc, xT, w1_words, w1_scales, w2_words, w2_sc
             shift_and_exp(slice(d, d + 1), parts[1])
         nc.vector.tensor_scalar_min(out=capped[:], in0=shifted[:, D - 1], scalar1=CAP)
         nc.scalar.activation(out=e[:, D - 1], in_=capped[:], func=ACT.Exp)
-        for ds, m in ((slice(0, D - 1), parts[0]), (slice(0, D - 2), parts[1]), (slice(D - 2, D - 1), parts[1]), (slice(D - 1, D), slice(0, N))):
-            nc.vector.tensor_tensor(out=eh[:, ds, m], in0=h_bank[:, ds, m], in1=e[:, ds, m], op=ALU.mult)
+        for d in range(D):
+            nc.vector.tensor_tensor(out=eh[:, d], in0=h_banks[d // 2][:, d % 2], in1=e[:, d], op=ALU.mult)
         den = psum.tile([P, V], F32, name="den")
         num = psum.tile([P, V], F32, name="num")
         for total, terms in ((den, e), (num, eh)):

@@ -25,7 +25,7 @@ GROUPS = 4
 SCALE_ROWS = 4
 LOADS = (4, 2, 1, 1)
 FIRST_FEATURES = 48
-CAP = 40.0
+DEPTH = 24.0
 
 
 def tile_picked_apool_none_e_kernel(tc, xT, w1_words, w1_scales, w2_words, w2_scales, offs, out):
@@ -50,7 +50,7 @@ def tile_picked_apool_none_e_kernel(tc, xT, w1_words, w1_scales, w2_words, w2_sc
             nc.gpsimd.memset(w_scales[a][:].rearrange("p z n -> p (z n)").bitcast(I32), 0)
         make_identity(nc, identity[:])
         warm = keep.tile([P, 1], F32, name="warm")
-        nc.scalar.activation(out=warm[:], in_=identity[:, 0:1], func=ACT.Exp)
+        nc.scalar.activation(out=warm[:], in_=identity[:, 0:1], func=ACT.Sigmoid)
 
         planes = []
         for count in LOADS:
@@ -141,22 +141,20 @@ def tile_picked_apool_none_e_kernel(tc, xT, w1_words, w1_scales, w2_words, w2_sc
         e = keep.tile([P, D, N], F32, name="e", tag="codes00", align_bytes=64)
         eh = keep.tile([P, D, N], F32, name="eh")
         parts = (slice(0, FIRST_FEATURES), slice(FIRST_FEATURES, N))
-        capped = keep.tile([P, N], F32, name="capped")
         for m in parts:
             nc.vector.tensor_reduce(out=top[:, m], in_=s_first[:, :, m].rearrange("p d m -> p m d"), axis=AX.X, op=ALU.max)
 
         def shift_and_exp(ds, m):
             spread = top[:, m].unsqueeze(1).to_broadcast([P, ds.stop - ds.start, m.stop - m.start])
             nc.vector.tensor_tensor(out=shifted[:, ds, m], in0=s_first[:, ds, m], in1=spread, op=ALU.subtract)
-            nc.scalar.activation(out=e[:, ds, m], in_=shifted[:, ds, m], func=ACT.Exp)
+            nc.scalar.activation(out=e[:, ds, m], in_=shifted[:, ds, m], func=ACT.Sigmoid, bias=-DEPTH)
 
         shift_and_exp(slice(0, D - 1), parts[0])
         for m in parts:
             nc.vector.tensor_tensor(out=shifted[:, D - 1, m], in0=s_last[:, m], in1=top[:, m], op=ALU.subtract)
         for d in range(D - 1):
             shift_and_exp(slice(d, d + 1), parts[1])
-        nc.vector.tensor_scalar_min(out=capped[:], in0=shifted[:, D - 1], scalar1=CAP)
-        nc.scalar.activation(out=e[:, D - 1], in_=capped[:], func=ACT.Exp)
+        nc.scalar.activation(out=e[:, D - 1], in_=shifted[:, D - 1], func=ACT.Sigmoid, bias=-DEPTH)
         for d in range(D):
             nc.vector.tensor_tensor(out=eh[:, d], in0=h_banks[d // 2][:, d % 2], in1=e[:, d], op=ALU.mult)
         den = psum.tile([P, V], F32, name="den")

@@ -24,7 +24,7 @@ D = S // V
 GROUPS = 4
 SCALE_ROWS = 4
 LOADS = (4, 2, 1, 1)
-FIRST_FEATURES = 48
+FIRST_FEATURES = 64
 DEPTH = 24.0
 
 
@@ -149,11 +149,11 @@ def tile_picked_apool_none_e_kernel(tc, xT, w1_words, w1_scales, w2_words, w2_sc
             nc.vector.tensor_tensor(out=shifted[:, ds, m], in0=s_first[:, ds, m], in1=spread, op=ALU.subtract)
             nc.scalar.activation(out=e[:, ds, m], in_=shifted[:, ds, m], func=ACT.Sigmoid, bias=-DEPTH)
 
-        shift_and_exp(slice(0, D - 1), parts[0])
-        for m in parts:
-            nc.vector.tensor_tensor(out=shifted[:, D - 1, m], in0=s_last[:, m], in1=top[:, m], op=ALU.subtract)
-        for d in range(D - 1):
+        shift_and_exp(slice(0, 2), parts[0])
+        for d in range(2):
             shift_and_exp(slice(d, d + 1), parts[1])
+        shift_and_exp(slice(2, 3), slice(0, N))
+        nc.vector.tensor_tensor(out=shifted[:, D - 1], in0=s_last[:], in1=top[:], op=ALU.subtract)
         nc.scalar.activation(out=e[:, D - 1], in_=shifted[:, D - 1], func=ACT.Sigmoid, bias=-DEPTH)
         for d in range(D):
             nc.vector.tensor_tensor(out=eh[:, d], in0=h_banks[d // 2][:, d % 2], in1=e[:, d], op=ALU.mult)

from contextlib import ExitStack

import concourse.mybir as mybir
from concourse.masks import make_identity

K, T, S, V, N = 1024, 2048, 512, 128, 128
FLOPS = 2 * 2 * K * N * S

F32 = mybir.dt.float32
BF16 = mybir.dt.bfloat16
U32 = mybir.dt.uint32
I32 = mybir.dt.int32
U16 = mybir.dt.uint16
U8 = mybir.dt.uint8
FP8X4 = mybir.dt.float8_e4m3fn_x4
ALU = mybir.AluOpType
ACT = mybir.ActivationFunctionType
AX = mybir.AxisListType

P = 128
PACK = 4
PASSES = K // (P * PACK)
D = S // V
GROUPS = 4
SCALE_ROWS = 4
LOADS = (4, 2, 1, 1)
FIRST_FEATURES = 64
DEPTH = 24.0


def tile_picked_apool_none_e_kernel(tc, xT, w1_words, w1_scales, w2_words, w2_scales, offs, out):
    nc = tc.nc
    with ExitStack() as ctx:
        keep = ctx.enter_context(tc.tile_pool(name="keep", bufs=1))
        psum = ctx.enter_context(tc.psum_pool(name="psum", bufs=1))

        offsets = keep.tile([P, S // 16], U16, name="offsets")
        x_rows = xT.rearrange("(z p j) t -> z p j t", z=PASSES, j=PACK)
        w_words = [keep.tile([P, PASSES, N], I32, name="w_words%d" % a, align_bytes=64) for a in range(2)]
        w_scales = [keep.tile([P, PASSES, N], U8, name="w_scales%d" % a, align_bytes=64) for a in range(2)]
        identity = keep.tile([P, P], F32, name="identity")

        def live(g):
            return slice(32 * g, 32 * g + SCALE_ROWS)

        def scale_rows(scales, g):
            return scales[:, SCALE_ROWS * g : SCALE_ROWS * (g + 1), :].rearrange("z r n -> r z n").bitcast(I32)

        for a in range(2):
            nc.gpsimd.memset(w_scales[a][:].rearrange("p z n -> p (z n)").bitcast(I32), 0)
        make_identity(nc, identity[:])
        warm = keep.tile([P, 1], F32, name="warm")
        nc.scalar.activation(out=warm[:], in_=identity[:, 0:1], func=ACT.Sigmoid)

        planes = []
        for count in LOADS:
            z, j0 = divmod(len(planes), PACK)
            rows = keep.tile([P, count, T], F32, name="rows%d%d" % (z, j0), tag="rows%d%d" % (z, j0), align_bytes=64)
            nc.sync.dma_start(out=rows[:], in_=x_rows[z, :, j0 : j0 + count, :])
            if not planes:
                nc.sync.dma_start(offsets[:], offs)
            planes.extend(rows[:, i, :] for i in range(count))
        for a, (words, scales) in enumerate(((w1_words, w1_scales), (w2_words, w2_scales))):
            nc.sync.dma_start(out=w_words[a][:], in_=words.rearrange("z p n r -> p z (n r)").bitcast(I32))
            for g in range(GROUPS):
                nc.sync.dma_start(out=w_scales[a][live(g)].bitcast(I32), in_=scale_rows(scales, g))

        s_first = psum.tile([P, D - 1, N], F32, name="s_first")
        s_last = psum.tile([P, N], F32, name="s_last")
        h_banks = [psum.tile([P, D // 2, N], F32, name="h_bank%d" % i) for i in range(2)]
        quantised = []
        laid_out = []

        def quantise(z, d, tag):
            codes, x_scales = quantised[z]
            codes.setdefault(d, keep.tile([P, V], U32, name="codes%d%d" % (z, d), tag=tag, align_bytes=64)[:])
            nc.vector.quantize_mx(out=codes[d].bitcast(FP8X4), scales=x_scales[:, d * V : (d + 1) * V], in_=laid_out[z][d].rearrange("p v j -> p (v j)"))

        half = S // 2
        for z in range(PASSES):
            x_scales = keep.tile([P, S], U8, name="x_scales%d" % z, align_bytes=64)
            if z == 0:
                runs = keep.tile([P, PACK, S], F32, name="runs", align_bytes=64)
                picked = keep.tile([P, S, PACK], BF16, name="picked", align_bytes=64)
                for j in range(PACK):
                    if j % 2 == 0:
                        nc.vector.tensor_copy(out=runs[:, j], in_=planes[j].indirect(offsets[:]))
                    else:
                        nc.scalar.activation(out=runs[:, j], in_=planes[j].indirect(offsets[:]), func=ACT.Copy)
                nc.vector.tensor_copy(out=picked[:], in_=runs[:].rearrange("p j s -> p s j"))
                pieces = [picked[:, d * V : (d + 1) * V] for d in range(D)]
            else:
                stepped = keep.tile([P, half, PACK], BF16, name="stepped", align_bytes=64)
                woven = [keep.tile([P, V, PACK], BF16, name="woven%d" % i, align_bytes=64) for i in range(D // 2)]
                pair = keep.tile([P, 2, half], F32, name="pair", align_bytes=64)
                for j in range(PACK):
                    plane = planes[PACK * z + j]
                    nc.vector.tensor_copy(out=stepped[:, :, j], in_=plane.indirect(offsets[:, : half // 16]))
                    if j < 2:
                        nc.scalar.activation(out=pair[:, j], in_=plane.indirect(offsets[:, half // 16 :]), func=ACT.Copy)
                        for i in range(D // 2) if j == 1 else []:
                            nc.vector.tensor_copy(out=woven[i][:, :, 0:2], in_=pair[:, :, i * V : (i + 1) * V].rearrange("p j s -> p s j"))
                        continue
                    run = keep.tile([P, half], BF16, name="run%d" % j, tag="run%d" % j, align_bytes=64)
                    parts_of_run = [slice(0, V), slice(V, 2 * V)] if j == PACK - 1 else [slice(0, half)]
                    for cols in parts_of_run:
                        nc.scalar.activation(out=run[:, cols], in_=plane.indirect(offsets[:, (half + cols.start) // 16 : (half + cols.stop) // 16]), func=ACT.Copy)
                    for i in range(D // 2):
                        nc.scalar.copy(out=woven[i][:, :, j], in_=run[:, i * V : (i + 1) * V])
                pieces = [stepped[:, :V], stepped[:, V:], woven[0][:], woven[1][:]]
            laid_out.append(pieces)
            quantised.append(({}, x_scales))
            for d in range(D - 1):
                quantise(z, d, "codes%d%d" % (z, d))
        quantise(0, D - 1, "run%d" % (PACK - 1))
        quantise(1, D - 1, "codes13")

        def one_pass(a, z, d, target, start, stop):
            codes, x_scales = quantised[z]
            nc.tensor.matmul_mx(
                out=target,
                lhsT=codes[d].bitcast(FP8X4),
                lhsT_scale=x_scales[:, d * V : (d + 1) * V],
                rhs=w_words[a][:, z, :].bitcast(FP8X4),
                rhs_scale=w_scales[a][:, z, :],
                start=start,
                stop=stop,
            )

        for z in range(PASSES):
            for d in range(D - 1):
                one_pass(0, z, d, s_first[:, d, :], z == 0 and d == 0, z == PASSES - 1 and d == D - 2)
        for z in range(PASSES):
            one_pass(0, z, D - 1, s_last[:], z == 0, z == PASSES - 1)
        for d in range(D):
            for z in range(PASSES):
                one_pass(1, z, d, h_banks[d // 2][:, d % 2, :], z == 0 and d % 2 == 0, z == PASSES - 1 and d % 2 == 1)

        top = keep.tile([P, N], F32, name="top")
        shifted = keep.tile([P, D, N], F32, name="shifted")
        e = keep.tile([P, D, N], F32, name="e", tag="codes00", align_bytes=64)
        eh = keep.tile([P, D, N], F32, name="eh")
        parts = (slice(0, FIRST_FEATURES), slice(FIRST_FEATURES, N))
        for m in parts:
            nc.vector.tensor_reduce(out=top[:, m], in_=s_first[:, :, m].rearrange("p d m -> p m d"), axis=AX.X, op=ALU.max)

        def shift_and_exp(ds, m):
            spread = top[:, m].unsqueeze(1).to_broadcast([P, ds.stop - ds.start, m.stop - m.start])
            nc.vector.tensor_tensor(out=shifted[:, ds, m], in0=s_first[:, ds, m], in1=spread, op=ALU.subtract)
            nc.scalar.activation(out=e[:, ds, m], in_=shifted[:, ds, m], func=ACT.Sigmoid, bias=-DEPTH)

        shift_and_exp(slice(0, 2), parts[0])
        for d in range(2):
            shift_and_exp(slice(d, d + 1), parts[1])
        shift_and_exp(slice(2, 3), slice(0, N))
        nc.vector.tensor_tensor(out=shifted[:, D - 1], in0=s_last[:], in1=top[:], op=ALU.subtract)
        nc.scalar.activation(out=e[:, D - 1], in_=shifted[:, D - 1], func=ACT.Sigmoid, bias=-DEPTH)
        for d in range(D):
            nc.vector.tensor_tensor(out=eh[:, d], in0=h_banks[d // 2][:, d % 2], in1=e[:, d], op=ALU.mult)
        den = psum.tile([P, V], F32, name="den")
        num = psum.tile([P, V], F32, name="num")
        for total, terms in ((den, e), (num, eh)):
            for d in range(D):
                nc.tensor.matmul(total[:], terms[:, d, :], identity[:], start=(d == 0), stop=(d == D - 1), is_transpose=True)
        inv = keep.tile([P, V], F32, name="inv")
        result = keep.tile([P, V], F32, name="result")
        halves = (slice(0, 3 * V // 4), slice(3 * V // 4, V))
        for v in halves:
            nc.vector.reciprocal(out=inv[:, v], in_=den[:, v])
        for v in halves:
            nc.vector.tensor_tensor(out=result[:, v], in0=num[:, v], in1=inv[:, v], op=ALU.mult)
        nc.sync.dma_start(out=out, in_=result[:])
